import numpy as np, ml_dtypes
CORES = [2,3,42,43,82,83,122,123]
N = 8
BF = ml_dtypes.bfloat16
S, U, NP, CAP, FO, RO = 2048, 4096, 256, 64, 2, 4
G = NP + FO * CAP
def parts(rng):
    x = rng.integers(0, 256, (N, 8, 16, S)); kd = rng.integers(0, 4096, (N, 16, U)); wt = rng.integers(0, 256, (N, 8, 16, 1))
    th = rng.integers(64, 208, (N, 8, 16, 1)); th = np.where(rng.random(th.shape) < 0.06, 256 * rng.integers(0, 2, th.shape), th)
    tau = rng.integers(900, 1700, (N, 8, 1, 1)) + rng.integers(-150, 151, (N, 8, 16, 1))
    return x, kd, wt, th, tau
def pack(x, kd, wt, th, tau):
    col = lambda a: np.ascontiguousarray(a.reshape(N, 128, 1)).astype(np.int32)
    return {"x0": np.ascontiguousarray(x.reshape(N, 128, S)).astype(np.float32).astype(BF), "kd": kd.astype(np.int32), "wt": col(wt), "th": col(th), "tau": col(tau)}
def draw_of(a):
    return (a * 4096 + S - 1) // S
def apart(rng, n):
    got = []; used = {0}
    for d in rng.permutation(np.arange(64, 4096 * S // (S + (RO - 1) * G))):
        v = {int(d) * (S + t * G) >> 12 for t in range(RO)}
        if len(v) == RO and not v & used:
            got.append(int(d)); used |= v
        if len(got) == n: break
    return np.array(got)
def columns_of(rng, h):
    z = h[:, None, :] // 16 + (np.arange(16)[None, :, None] < h[:, None, :] % 16)
    a, b = z[:, ::2], z[:, 1::2]; s = rng.integers(0, np.minimum(a, 255 - b) + 1); z = np.concatenate([a - s, b + s], axis=1)
    return np.take_along_axis(z, np.argsort(rng.random(z.shape), axis=1), 1)
def setup_inputs(rng):
    return pack(*parts(rng))
def setup_inputs_corners(rng):
    x, kd, wt, th, tau = parts(rng)
    kd = np.where(rng.random(kd.shape) < 0.3, 4095 * rng.integers(0, 2, kd.shape), kd); ui = (613 * np.arange(NP)) & (U - 1)
    for a in range(N):
        o = 2 + rng.permutation(S - 2); o = np.concatenate([[0], o[:NP - 1], [1], o[NP - 1:]]); p, q = o[:NP], o[NP:2 * NP]
        first = rng.random((16, NP)) < 0.5; first[0] = True; first[15] = False
        kd[a][:, ui] = draw_of(np.where(first, p[None, :], q[None, :]))
        cnt = rng.permutation(np.array([0, 1, CAP - 1, CAP, CAP + 1, NP]))
        for g in range(6):
            m = rng.permutation(NP)[:int(cnt[g])]
            wt[a, g] = 0; th[a, g] = 256 * rng.integers(0, 2, (16, 1)); th[a, g, 0] = 0
            tau[a, g] = rng.choice(np.array([0, 1, 1000, 1500, 4079, 4080]), (16, 1)); tau[a, g, 0] = 4079
            x[a, g][:, q] = x[a, g][:, p]; x[a, g][:, p[m]] = 0; x[a, g][:, q[m]] = 255
        wt[a, 6] = 255; th[a, 6] = rng.choice(np.array([0, 1, 128, 255, 256]), (16, 1)); tau[a, 6] = rng.choice(np.array([0, 1300, 4080]), (16, 1))
        th[a, 7] = 256
    return pack(x, kd, wt, th, tau)
def setup_inputs_deep(rng):
    x, kd, wt, th, tau = parts(rng)
    near = 4095 - np.floor(300 * rng.random(kd.shape) ** 2).astype(np.int64)
    kd = np.where(rng.random(kd.shape) < 0.7, near, kd); th = rng.integers(90, 140, th.shape)
    tau = np.minimum(rng.choice(np.array([0, 300, 600, 900, 1200, 4080]), (N, 8, 1, 1)) + rng.integers(0, 200, (N, 8, 16, 1)), 4080)
    tau[:, 2] = 4080; tau[:, 5] = 0
    return pack(x, kd, wt, th, tau)
def setup_inputs_ends(rng):
    x = 255 * rng.integers(0, 2, (N, 8, 16, S)); x = np.where(rng.random((N, 8, 1, S)) < 0.4, 255 * rng.integers(0, 2, (N, 8, 1, S)), x)
    wt = 255 * rng.integers(0, 2, (N, 8, 16, 1)); sh = wt.shape
    th = np.where(rng.random(sh) < 0.75, 256 * rng.integers(0, 2, sh), rng.choice(np.array([1, 128, 255]), sh))
    tau = np.where(rng.random(sh) < 0.7, 4080 * rng.integers(0, 2, sh), 255 * rng.integers(0, 17, sh))
    end = (rng.random((N, 1, U)) < 0.5) | (rng.random((N, 16, U)) < 0.5)
    kd = np.where(end, 4095 * rng.integers(0, 2, (N, 16, U)), rng.integers(0, 4096, (N, 16, U)))
    bits = rng.integers(0, 2, (N, 1, S)); bits[..., 0] = 0; bits[..., S - 1] = 1; bits[..., S - G] = 1; bits[..., S - G + 1] = 0; bits[..., S - G + NP - 1] = 1
    x[:, 7] = 255 * bits; wt[:, 7] = 255
    th[:, 7] = 256 * rng.integers(0, 2, (N, 16, 1)); th[:, 7, 0] = 0; th[:, 7, 1] = 256; th[:, 7, 14] = 0; th[:, 7, 15] = 0
    tau[:, 7] = 4080 * rng.integers(0, 2, (N, 16, 1)); tau[:, 7, 0] = 4080; tau[:, 7, 14] = 4080; tau[:, 7, 15] = 0
    i = 613 * np.arange(NP); both = np.unique(np.concatenate([i & (U - 1), (i + 16 * 255 * 255) & (U - 1)]))
    kd[:, :, both] = 4095 * rng.integers(0, 2, (N, 16, len(both))); kd[:, 1, both] = 4095; kd[:, 15, both] = 0; kd[:, 0, 0] = 0
    e = np.array([613 * (CAP - 1), 613 * (NP - 1)]); e = np.concatenate([e, e + 16 * 255 * 255]) & (U - 1)
    kd[:, :, e] = 4095; kd[:, 15, e] = 0; kd[:, 0, (e + 1) & (U - 1)] = 4095
    return pack(x, kd, wt, th, tau)
def setup_inputs_spread(rng):
    x, kd, wt, th, tau = parts(rng); sh = wt.shape
    x = np.minimum(np.floor(np.exp2(8 * rng.random((N, 8, 1, S))) * rng.random((N, 8, 16, S))), 255).astype(np.int64)
    kd = np.minimum(np.floor(4096 * rng.random((N, 16, U)) ** np.exp2(rng.integers(-2, 3, (N, 1, U)))), 4095).astype(np.int64)
    wt = np.minimum(np.floor(np.exp2(8 * rng.random(sh))) - 1, 255).astype(np.int64); wt[:, :, 3] = 255
    th = np.where(rng.random(sh) < 0.7, np.minimum(np.floor(np.exp2(8.01 * rng.random(sh))) - 1, 256), rng.integers(0, 257, sh)).astype(np.int64)
    tau = np.where(rng.random(sh) < 0.5, np.minimum(np.floor(np.exp2(12 * rng.random(sh))) - 1, 4080), rng.integers(200, 2200, sh)).astype(np.int64)
    return pack(x, kd, wt, th, tau)
def setup_inputs_turns(rng):
    x, kd, wt, th, tau = parts(rng); wt[...] = 0; ui = (613 * np.arange(NP)) & (U - 1); n = 20; tight = np.arange(n) % 2 == 0
    own = np.concatenate([np.arange(4), np.full(CAP - 2, 4), 5 + np.arange(NP - CAP - 2) % (n - 5)])
    pat = np.zeros((6, n), bool); pat[1, 0] = True; pat[2, [0, 4]] = True; pat[3, [0, 1, 4]] = True; pat[4, [0, 1, 2, 4]] = True; pat[5] = True
    q = rng.permutation(N)
    for a in range(N):
        d = apart(rng, n); c = rng.permutation(own); size = np.bincount(c, minlength=n)
        first = rng.random((16, NP)) < 0.5; first[0] = True; first[15] = False
        kd[a][:, ui] = np.where(first, d[c][None, :], 0)
        opt = rng.integers(0, 7, (RO, 8))
        if a == q[0]:
            opt[0] = rng.permutation(np.array([0, 1, 1, 1, 2, 3, 4, 5])); opt[1] = 0; opt[2] = rng.integers(1, 6, 8)
        if a == q[1]:
            opt[1] = 5; opt[2] = rng.integers(1, 6, 8)
        go = np.where((opt == 6)[..., None], rng.random((RO, 8, n)) < 0.5, pat[np.minimum(opt, 5)])
        least = rng.permutation(np.concatenate([np.array([0, 64, 2047, 2048, 4064]), rng.integers(100, 4065, 3)])); row = rng.integers(0, 16, 8)
        th[a, :, :, 0] = rng.choice(np.array([0, 0, 1, 128, 255, 256]), (8, 16))
        tau[a, :, :, 0] = np.minimum(least[:, None] + rng.choice(np.array([0, 0, 1, 15, 500, 4080]), (8, 16)), 4080)
        th[a, np.arange(8), row, 0] = 0; tau[a, np.arange(8), row, 0] = least
        count = 0
        for t in range(RO):
            lim = (least + (count & 15))[:, None]; v = (d * (S + t * G)) >> 12
            over = np.where(tight, 1, 1 + np.floor((4080 - lim) * rng.random((8, n))).astype(np.int64))
            under = np.where(tight, 0, np.floor((lim + 1) * rng.random((8, n))).astype(np.int64))
            x[a][:, :, v] = columns_of(rng, np.where(go[t], lim + over, lim - under))
            count = int(np.sum(size * go[t]))
        x[a][:, :, 0] = 0
    return pack(x, kd, wt, th, tau)
def check_inputs(d):
    bad = []
    for k, lo, hi in (("x0", 0, 255), ("kd", 0, 4095), ("wt", 0, 255), ("th", 0, 256), ("tau", 0, 4080)):
        a = np.asarray(d[k]).astype(np.float64)
        if not (np.all(a >= lo) and np.all(a <= hi) and np.all(a == np.floor(a))): bad.append("range of " + k)
    return bad
def reference(x0, kd, wt, th, tau):
    tot = S + RO * G
    X = np.zeros((N, 8, 16, tot), np.int64); X[..., :S] = x0.astype(np.float32).astype(np.int64).reshape(N, 8, 16, S)
    A = np.zeros((N, 8, 16, tot), np.int64); A[...] = np.arange(tot)
    tb = kd.astype(np.int64); w = wt.astype(np.int64).reshape(N, 8, 16, 1); lim = tau.astype(np.int64).reshape(N, 8, 16, 1); thr = th.astype(np.int64).reshape(N, 8, 16, 1, 1)
    C = [0] * N
    for t in range(RO):
        B = S + t * G
        u = (np.sum(w * X[..., B - G:B - G + NP], axis=2) + 613 * np.arange(NP)) & (U - 1)
        mail = []
        for a in range(N):
            e = (tb[a][:, u[a]] * B) >> 12
            ix = np.ascontiguousarray(e.transpose(1, 2, 0)).reshape(8, 1, NP * 16)
            xe = np.take_along_axis(X[a], ix, 2).reshape(8, 16, NP, 16); ne = np.take_along_axis(A[a], ix, 2).reshape(8, 16, NP, 16)
            m = xe >= thr[a]
            lo = np.min(np.where(m, ne, tot), axis=3); hi = np.max(np.where(m, ne, -1), axis=3); none = hi < 0
            lo = np.where(none, ne[..., 0], lo); hi = np.where(none, ne[..., 0], hi)
            xl = np.take_along_axis(X[a], lo.reshape(8, 1, 16 * NP), 2).reshape(8, 16, 16, NP)
            xh = np.take_along_axis(X[a], hi.reshape(8, 1, 16 * NP), 2).reshape(8, 16, 16, NP)
            D = np.sum(np.abs(xl - xh), axis=1)
            far = D > lim[a] + (C[a] & 15)
            A[a, :, :, B:B + NP] = np.where(far, np.arange(B, B + NP), lo)
            nx = (np.max(xl, axis=2) + np.min(xh, axis=2)) >> 1
            X[a, :, :, B:B + NP] = nx
            c = np.any(far, axis=1)
            C[a] = int(np.sum(c))
            o = np.argsort(np.where(c, 0, 1), axis=1, kind="stable")[:, :CAP]
            mail.append(np.where(np.take_along_axis(c, o, 1)[:, None, :], np.take_along_axis(nx, o[:, None, :], 2), 0))
        for a in range(N):
            for f in range(FO):
                q = (a - 1 - (FO * t + f) % (N - 1)) % N; b = B + NP + f * CAP
                X[a, :, :, b:b + CAP] = mail[q]
    return {"ya": A[..., S:].reshape(N, 128, RO * G).astype(np.float32), "yx": X[..., S:].reshape(N, 128, RO * G).astype(np.float32).astype(BF)}

@@ -1,0 +1,481 @@
+from concourse.bass import DstId, RemoteDMATransfer
+from concourse.mybir import AluOpType, ActivationFunctionType, AxisListType
+
+N, S, U, NP, CAP, FO, RO = 8, 2048, 4096, 256, 64, 2, 4
+G = NP + FO * CAP
+TOT = S + RO * G
+CH = [(0, 64), (64, 128), (128, 192), (192, 256)]
+UH = [(0, 256)]
+XHV, XLV = ((3, 0), (3, 1), (2, 0)), ()
+SUB = {3: [(0, 32), (32, 64)]}
+P = max(b - a for a, b in CH)
+E = 16 * P
+DEP = 4
+WAKE = 0.1
+GCY, TCY, MLAT = 1.6, 0.001, 3.0
+DELTA = 0.15
+BK = {'-:9': -10.7, 'ab:0': 3.0, 'ab:1': -3.6, 'ab:2': -7.5, 'ab:3': -3.9, 'ad:0': -5.5, 'ad:1': -2.3, 'ad:2': 6.0, 'ad:3': -6.1,
+      'ci:9': -0.1, 'cj:9': -1.8, 'cs:9': 0.8, 'e:3': -3.6, 'fb:0': 1.8, 'fb:1': 2.2, 'fb:2': 3.0, 'fb:3': -8.0, 'hk:0': 4.4, 'hk:1': 5.5,
+      'hk:2': -5.7, 'hk:3': -10.1, 'hl:0': -3.5, 'hl:1': 0.6, 'hl:2': -2.9, 'hl:3': 9.5, 'hs:0': -0.4, 'hs:1': -3.5, 'hs:2': 0.1,
+      'hs:3': -3.7, 'kw:0': -0.2, 'kw:1': 3.9, 'kw:2': -6.7, 'kw:3': 7.1, 'kw:9': 3.1, 'lk:0': -1.9, 'lk:1': -0.1, 'lk:2': 0.2,
+      'lk:3': 3.9, 'lof:0': -0.4, 'lof:1': 0.7, 'lof:2': -2.1, 'lof:3': 7.8, 'ls:0': -3.3, 'ls:1': -3.7, 'ls:2': -4.9, 'ls:3': -8.8,
+      'mn:0': 7.7, 'mn:1': -6.3, 'mn:2': -7.2, 'mn:3': -5.1, 'ms:0': 3.5, 'ms:1': -2.7, 'ms:2': -16.2, 'ms:3': 0.6, 'mw:9': -0.2,
+      'n:0': -1.6, 'n:1': 1.4, 'n:2': 2.0, 'n:3': 4.5, 'n:9': -6.8, 'nb:9': -6.5, 'nc:9': 7.7, 'no:0': -3.2, 'no:1': -0.1, 'no:2': -2.4,
+      'no:3': -1.3, 'off:9': 1.2, 'om:9': 6.5, 'pd:0': -7.6, 'pd:1': -2.5, 'pd:2': -14.9, 'pd:3': 8.0, 'pl:0': -7.5, 'pl:1': -11.6,
+      'pl:2': -2.2, 'pl:3': 3.9, 'pm:9': 7.7, 'pq:0': -3.0, 'pq:1': -1.6, 'pq:2': 2.1, 'pq:3': 10.3, 'pw:3': -0.7, 'r:0': 3.9, 'r:1': 6.4,
+      'r:2': 3.5, 'r:3': 1.6, 'ui:3': 2.7, 'uj:3': -1.5, 'uo:3': 2.9, 'w:0': 2.0, 'w:1': -3.7, 'w:2': -4.6, 'w:3': -2.9, 'xb:0': 7.8,
+      'xb:1': 5.9, 'xb:2': -5.1, 'xb:3': 1.0, 'xb:9': 2.6, 'xh:0': -3.4, 'xh:1': 3.6, 'xh:2': -3.8, 'xh:3': 4.1, 'xl:0': -6.2,
+      'xl:1': -6.8, 'xl:2': 0.4, 'xl:3': 6.0, 'yf:3': -4.6}
+STATS = {}
+MAGIC = 12582912.0
+F16 = "float16"
+
+COLS = ["wtf", "thf", "ntau", "prf", "pixf", "cs", "ia0", "ia1", "iz0", "iz1", "nb0", "nb1", "nb2", "nb3"]
+
+SCRATCH = {
+    "xb": ("sbuf", [128, TOT], "bfloat16"),
+    "kw": ("sbuf", [128, TOT], "float32"),
+    "kdw": ("sbuf", [128, U], "int32"),
+    "ab": ("sbuf", [128, RO * G], "float32"),
+    "onesb": ("sbuf", [128, 512], "bfloat16"),
+    "io16": ("sbuf", [128, 512], F16),
+    "n8h": ("sbuf", [128, S], F16),
+    "rneg": ("sbuf", [128, E], "bfloat16"),
+    "rpos": ("sbuf", [128, E], "bfloat16"),
+    "g2a": ("sbuf", [128, 144], "bfloat16"),
+    "g2": ("sbuf", [128, 144], "bfloat16"),
+    "l1": ("sbuf", [128, 144], "bfloat16"),
+    "lw": ("sbuf", [128, 144], "bfloat16"),
+    "ib": ("sbuf", [128, 128], "bfloat16"),
+    "nib": ("sbuf", [128, 128], "bfloat16"),
+    "hib": ("sbuf", [128, 128], "bfloat16"),
+    "nif": ("sbuf", [128, 128], "float32"),
+    "ih": ("sbuf", [128, 128], F16),
+    "nih": ("sbuf", [128, 128], F16),
+    "i84h": ("sbuf", [128, 128], F16),
+    "c17": ("sbuf", [128, P], F16),
+    "cq": ("sbuf", [128, P], "bfloat16"),
+    "wti": ("sbuf", [128, 1], "int32"), "thi": ("sbuf", [128, 1], "int32"), "taui": ("sbuf", [128, 1], "int32"),
+    "fc": ("sbuf", [128, len(COLS)], "float32"),
+    "pix": ("sbuf", [128, 1], "int32"), "pr": ("sbuf", [128, 1], "int32"),
+    "c16": ("sbuf", [128, 16], "float32"), "icf": ("sbuf", [128, 16], "float32"),
+    "uc": ("sbuf", [128, 16], "float32"),
+    "ui": ("sbuf", [128, 16], "int32"), "uj": ("sbuf", [128, 16], "int32"), "uo": ("sbuf", [128, 16], "uint16"),
+    "n8": ("sbuf", [128, G], "bfloat16"),
+    "uut": ("sbuf", [128, 128], "bfloat16"), "qm": ("sbuf", [128, 128], "bfloat16"), "mask": ("sbuf", [128, 128], F16),
+    "onh": ("sbuf", [128, 128], F16), "nonh": ("sbuf", [128, 128], F16), "selh": ("sbuf", [128, 8], F16),
+    "pm": ("psum", [128, 512], "float32"),
+    "off": ("sbuf", [128, 16], "uint16"),
+    "ci": ("sbuf", [128, 1], "int32"), "cj": ("sbuf", [128, 1], "int32"),
+    "pl0": ("psum", [128, 512], "float32"), "pl1": ("psum", [128, 512], "float32"),
+    "pq": ("psum", [128, 512], "float32"), "pw": ("psum", [128, 512], "float32"),
+}
+for _b in range(2):
+    for _n in ("nc", "om", "di", "dz", "mz"):
+        SCRATCH["%s%d" % (_n, _b)] = ("sbuf", [128, 128], F16)
+    SCRATCH["yf%d" % _b] = ("sbuf", [128, NP], "float32")
+    SCRATCH["e16%d" % _b] = ("sbuf", [128, NP], "uint16")
+    SCRATCH["r%d" % _b] = ("sbuf", [128, NP], "bfloat16")
+    SCRATCH["lof%d" % _b] = ("sbuf", [128, NP], "float32")
+    SCRATCH["fb%d" % _b] = ("sbuf", [128, NP], "float32")
+for _b in range(DEP):
+    SCRATCH["hk%d" % _b] = ("sbuf", [128, E], F16)
+    SCRATCH["hs%d" % _b] = ("sbuf", [128, E], F16)
+    SCRATCH["lk%d" % _b] = ("sbuf", [128, E], "float32")
+    SCRATCH["ls%d" % _b] = ("sbuf", [128, E], "float32")
+    for _n in ("xl", "xh", "ms", "mn", "ad"):
+        SCRATCH["%s%d" % (_n, _b)] = ("sbuf", [128, E], "bfloat16")
+    SCRATCH["no%d" % _b] = ("sbuf", [128, P], F16)
+    SCRATCH["w%d" % _b] = ("sbuf", [128, P], "float32")
+    SCRATCH["hl%d" % _b] = ("sbuf", [128, 2 * P], "uint16")
+for _t in range(RO):
+    if _t < 3:
+        SCRATCH["pd%d" % _t] = ("psum", [128, 512], "float32")
+    SCRATCH["mw%d" % _t] = ("sbuf", [128, 768], "bfloat16")
+
+SEMAPHORES = (["sv", "ss", "st", "sg", "rl"] + ["ma%d" % t for t in range(RO)] + ["lx%d" % b for b in range(4)]
+              + ["lk"] + ["lc%d" % b for b in range(3)] + ["out%d" % b for b in range(24)])
+
+
+def rank_program(g, core, T, topo):
+    rank = T.rank_of(core)
+    if rank is None:
+        return
+    A, AF = AluOpType, ActivationFunctionType
+    queues = {"V": g.vector, "S": g.scalar, "T": g.tensor, "G": g, "Y": g.sync}
+    own = {"V": "sv", "S": "ss", "T": "st", "G": "sg"}
+    CY = 0.001
+    ch = [8]
+
+    nodes, acc = [], {}
+
+    def R(name, c0, c1, step=1):
+        if name in COLS:
+            k = COLS.index(name)
+            return (T.fc[:, k:k + 1], [("fc", k, k + 1)])
+        return (T[name][:, c0:c1:step] if step > 1 else T[name][:, c0:c1], [(name, c0, c1)])
+
+    def IND(win, off):
+        return (win[0].indirect(off[0]), win[1] + off[1])
+
+    def clash(a, q, name, c0, c1, w):
+        if a[0] < c1 and c0 < a[1] and (w or a[2]):
+            return True
+        return name[:2] in ("pd", "pl", "pq", "pw", "pm") and a[3] != q
+
+    def node(q, fns, ins, outs, cost, sem=None, inc=1, preds=(), lat=0.0):
+        k, ps = len(nodes), set(preds)
+        kind = outs[0][0].strip("0123456789") if outs else "-"
+        for regs, w in ((ins, False), (outs, True)):
+            for name, c0, c1 in regs:
+                for a in acc.get(name, ()):
+                    if a[4] != k and clash(a, q, name, c0, c1, w):
+                        ps.add(a[4])
+        for regs, w in ((ins, False), (outs, True)):
+            for name, c0, c1 in regs:
+                lst = acc.setdefault(name, [])
+                if w:
+                    lst[:] = [a for a in lst if not (c0 <= a[0] and a[1] <= c1)]
+                lst.append((c0, c1, w, q, k))
+        nodes.append({"q": q, "fns": fns, "cost": cost, "sem": sem or own[q], "inc": inc, "ps": sorted(ps), "lat": lat, "kind": kind + ":%d" % ch[0]})
+        return k
+
+    def cat(*rs):
+        return [x for r_ in rs for x in r_[1]]
+
+    def col(c):
+        return R(c, 0, 1)[1]
+
+    def gat(n):
+        return 0.06 + n * GCY * CY
+
+    def size(r_, j=0):
+        return max(64, r_[1][j][2] - r_[1][j][1])
+
+    def copy(out, in_, n=None):
+        node("V", [lambda: g.vector.tensor_copy(out[0], in_[0])], in_[1], out[1], gat(n) if n else size(out) * CY)
+
+    def ts(out, in0, s1, s2, op0, op1=None, n=None, half=False):
+        ins = list(in0[1])
+        if isinstance(s1, str):
+            ins += col(s1)
+            s1 = R(s1, 0, 1)[0]
+        if isinstance(s2, str):
+            ins += col(s2)
+            s2 = R(s2, 0, 1)[0]
+        cost = gat(n) if n else (max(64, size(out) / 2) if half else size(out)) * CY
+        if op1 is None:
+            node("V", [lambda: g.vector.tensor_scalar(out[0], in0[0], s1, None, op0)], ins, out[1], cost)
+        else:
+            node("V", [lambda: g.vector.tensor_scalar(out[0], in0[0], s1, s2, op0, op1)], ins, out[1], cost)
+
+    def tt(out, in0, in1, op):
+        ps = any(x[1][0][0][:2] in ("pl", "pw", "pm") for x in (in0, in1))
+        node("V", [lambda: g.vector.tensor_tensor(out[0], in0[0], in1[0], op)], cat(in0, in1), out[1], size(out) * (1 if ps else 2) * CY)
+
+    def scan(out, d0, d1, init, op0, op1, half=True):
+        first, ins = init, cat(d0, d1)
+        if isinstance(init, tuple):
+            first, ins = init[0], ins + init[1]
+        node("V", [lambda: g.vector.tensor_tensor_scan(out[0], d0[0], d1[0], first, op0, op1)], ins, out[1],
+             max(64, size(out) * (0.5 if half else 1)) * CY)
+
+    def fill(out, c):
+        node("V", [lambda: g.vector.memset(out[0], c)], [], out[1], size(out) * 0.5 * CY)
+
+    def act(out, in_, func, bias=None, scale=None, n=None):
+        kw, ins = {}, list(in_[1])
+        if isinstance(bias, str):
+            ins += col(bias)
+            kw["bias"] = R(bias, 0, 1)[0]
+        elif bias is not None:
+            kw["bias"] = bias
+        if isinstance(scale, str):
+            ins += col(scale)
+            kw["scale"] = R(scale, 0, 1)[0]
+        elif scale is not None:
+            kw["scale"] = scale
+        node("S", [lambda: g.scalar.activation(out[0], in_[0], func, **kw)], ins, out[1], gat(n) if n else 0.04 + size(out) * CY)
+
+    def group(out, pairs):
+        fns, ins, cost = [], [], 0.0
+        for j, (l, r_) in enumerate(pairs):
+            fns.append(lambda l=l, r_=r_, j=j: g.tensor.matmul(out[0], l[0], r_[0], j == 0, j == len(pairs) - 1))
+            ins += [x for x in l[1] + r_[1] if x not in ins]
+            cost += max(64, out[1][0][2] - out[1][0][1]) * TCY * (4 if l[1][0][0] == "nif" else 1)
+        node("T", fns, ins, out[1], cost)
+
+    def wrap(out, mat, rname, c0, c1):
+        group(out, [(R(mat, 15 - r_, 143 - r_), R(rname, c0 + r_, c1, 16)) for r_ in range(16)])
+
+    def load(q, pairs, sem, outs, lat):
+        node(q, [lambda o=o, i=i: queues[q].dma_start(o, i) for o, i in pairs], [], outs, 0.06 * len(pairs), sem=sem, inc=16, lat=lat)
+
+    load("Y", [(T.thi[:, 0:1], T.th[:, 0:1])], "lc1", col("thi"), 2.0)
+    load("S", [(T.wti[:, 0:1], T.wt[:, 0:1])], "lc0", col("wti"), 2.0)
+    for j, b in enumerate((3, 0, 1, 2)):
+        load("Y", [(T.xb[:, 512 * b:512 * b + 512], T.x0[:, 512 * b:512 * b + 512])], "lx%d" % b,
+             [("xb", 512 * b, 512 * b + 512)], 2.5 + 0.8 * j)
+    load("S", [(T.kdw[16 * k:16 * k + 16, :], T.kd[:, :]) for k in range(8)], "lk", [("kdw", 0, U)], 10.0)
+    load("Y", [(T.taui[:, 0:1], T.tau[:, 0:1])], "lc2", col("taui"), 6.0)
+
+    fill(R("onesb", 0, 512), 1.0)
+
+    def asel(out, in_, pattern, op, base, cm):
+        node("G", [lambda: g.affine_select(out[0], in_[0], pattern, op, 0.0, base, cm)], in_[1], out[1], 0.5)
+
+    def iota(name, c0, c1, pattern, base, cm):
+        node("G", [lambda: g.iota(T[name][:, c0:c1], pattern, base, cm, allow_small_or_imprecise_dtypes=True)], [], [(name, c0, c1)],
+             0.15 + 2 * (c1 - c0) * CY)
+    asel(R("ib", 0, 128), R("onesb", 0, 128), [[-1, 128]], A.is_equal, 0, 1)
+    asel(R("g2a", 0, 144), R("onesb", 0, 144), [[-16, 9], [0, 16]], A.is_ge, 0, 1)
+    asel(R("g2", 0, 144), R("g2a", 0, 144), [[16, 9], [0, 16]], A.is_ge, 15, -1)
+    asel(R("l1", 0, 144), R("g2", 0, 144), [[0, 9], [1, 16]], A.is_equal, -15, 0)
+    node("G", [lambda: g.iota(T.pix[:, 0:1], [[0, 1]], 0, 1)], [], col("pix"), 0.15)
+    iota("c16", 0, 16, [[16, 16]], 0, 0)
+    asel(R("uut", 0, 128), R("onesb", 0, 128), [[1, 128]], A.is_ge, 0, -1)
+    asel(R("qm", 0, 128), R("onesb", 0, 128), [[0, 8], [-1, 16]], A.is_equal, 0, 1)
+    for b in range(3):
+        iota("ab", 512 * b, 512 * b + 512, [[1, 512]], S + 512 * b, 0)
+    scan(R("io16", 0, 512), R("onesb", 0, 512), R("onesb", 0, 512), -1.0, A.mult, A.add)
+    copy(R("ih", 0, 128), R("ib", 0, 128))
+    ts(R("nih", 0, 128), R("ib", 0, 128), -1.0, None, A.mult)
+    copy(R("thf", 0, 1), R("thi", 0, 1))
+    copy(R("wtf", 0, 1), R("wti", 0, 1))
+    act(R("lw", 0, 144), R("l1", 0, 144), AF.Copy, scale="wtf")
+    ts(R("pr", 0, 1), R("pix", 0, 1), 15, None, A.bitwise_and)
+    copy(R("prf", 0, 1), R("pr", 0, 1))
+    ts(R("icf", 0, 16), R("c16", 0, 16), "prf", None, A.add)
+    ts(R("uc", 0, 16), R("icf", 0, 16), 613.0, None, A.mult)
+
+    def next_u(t, i0, i1):
+        B = S + G * t
+        c0, c1 = i0 // 16, i1 // 16
+        n = str(t % 2)
+        wrap(R("pw", c0, c1), "lw", "xb", B - G + i0, B - G + i1)
+        tt(R("ui", c0, c1), R("pw", c0, c1), R("uc", c0, c1), A.add)
+        ts(R("uj", c0, c1), R("ui", c0, c1), 4095, None, A.bitwise_and)
+        copy(R("uo", c0, c1), R("uj", c0, c1))
+        ts(R("yf" + n, i0, i1), IND(R("kdw", 0, U), R("uo", c0, c1)), B / 4096.0, -0.484375, A.mult, A.add, n=i1 - i0)
+        ts(R("e16" + n, i0, i1), R("yf" + n, i0, i1), MAGIC, -MAGIC, A.add, A.add)
+
+    for b in (3, 0, 1, 2):
+        c0 = 512 * b
+        ts(R("n8h", c0, c0 + 512), R("xb", c0, c0 + 512), "thf", 8192.0, A.is_lt, A.mult, half=True)
+        group(R("pd%d" % (b % 3), 0, 512), [(R("ih", 0, 128), R("io16", 0, 512)), (R("nih", 0, 128), R("n8h", c0, c0 + 512))])
+        act(R("kw", c0, c0 + 512), R("pd%d" % (b % 3), 0, 512), AF.Copy, bias=float(c0))
+    for i0, i1 in UH:
+        next_u(0, i0, i1)
+    fill(R("rneg", 0, E), 0.0)
+    fill(R("rpos", 0, E), 0.0)
+    fill(R("rneg", 0, E, 16), -32768.0)
+    fill(R("rpos", 0, E, 16), 32768.0)
+    ts(R("i84h", 0, 128), R("ib", 0, 128), 8448.0, None, A.mult)
+    ts(R("c17", 0, P), R("onesb", 0, P), 1792.0, None, A.mult)
+    act(R("nif", 0, 128), R("ib", 0, 128), AF.Copy, scale=-1.0)
+    act(R("nib", 0, 128), R("ib", 0, 128), AF.Copy, scale=-1.0)
+    act(R("hib", 0, 128), R("ib", 0, 128), AF.Copy, scale=0.5)
+    fill(R("cq", 0, P), -0.25)
+    ts(R("ntau", 0, 1), R("taui", 0, 1), -8192.0, None, A.mult)
+    copy(R("nb0", 0, 1), R("ntau", 0, 1))
+    copy(R("pixf", 0, 1), R("pix", 0, 1))
+    copy(R("onh", 0, 128), R("onesb", 0, 128))
+    ts(R("nonh", 0, 128), R("onesb", 0, 128), -1.0, None, A.mult)
+    group(R("pm", 0, 128), [(R("qm", 0, 128), R("qm", 0, 128))])
+    copy(R("mask", 0, 128), R("pm", 0, 128))
+    copy(R("selh", 0, 8), R("g2", 0, 128, 16))
+    for j in range(2):
+        n = str(j)
+        ts(R("ia" + n, 0, 1), R("pixf", 0, 1), 128.0 * j, None, A.add)
+        ts(R("iz" + n, 0, 1), R("pixf", 0, 1), 256.0 + 128.0 * j, None, A.add)
+        ts(R("di" + n, 0, 128), R("ih", 0, 128), "ia" + n, None, A.mult)
+        ts(R("dz" + n, 0, 128), R("ih", 0, 128), "iz" + n, None, A.mult)
+        tt(R("mz" + n, 0, 128), R("dz" + n, 0, 128), R("uut", 0, 128), A.subtract)
+    for t in range(RO):
+        fill(R("mw%d" % t, 0, CAP), 0.0)
+
+    outs_used, pieces, uses = [0], [0], [0]
+
+    def store(out, in_):
+        node("Y", [lambda: g.sync.dma_start(out, in_[0])], in_[1], [], 0.06, sem="out%d" % outs_used[0], inc=16, lat=2.0)
+        outs_used[0] += 1
+
+    def send(t, B):
+        trs = []
+        for f in range(FO):
+            to = T.cores[(rank + 1 + (FO * t + f) % (N - 1)) % N]
+            rid, pid, _ = topo.addr(to)
+            b = B + NP + CAP * f
+            m = 0
+            for e in topo.engines(core, to)[4 * f:4 * f + 4]:
+                m |= 1 << e
+            trs.append(RemoteDMATransfer(dst_ids=[DstId(rid=rid, pnc=pid)], dma_engine_mask=m, remote_sem=T.sem["ma%d" % t],
+                                         srcs=[T["mw%d" % t][:, 0:CAP]], dsts=[T.xb[:, b:b + CAP]]))
+        g.remote_dma_fused(trs, local_sem=T.sem.rl)
+
+    for t in range(RO):
+        B, Y = S + G * t, G * t
+        gp = str(t % 2)
+        last = t == RO - 1
+        st = []
+        for c, (i0, i1) in enumerate(CH):
+            n, e = i1 - i0, 16 * (i1 - i0)
+            st.append((c, i0, i1, n, e, str(uses[0] % DEP), str(uses[0] % 2)))
+            uses[0] += 1
+
+        def names(c, i0, i1, n, e, b, l):
+            ch[0] = c
+            kids = IND(R("kw", 0, B), R("e16" + gp, i0, i1))
+            act(R("lk" + b, 0, e), kids, AF.Abs, n=e)
+            ts(R("hk" + b, 0, e), kids, -1792.0, -2048.0, A.add, A.max, n=e)
+            scan(R("hs" + b, 0, e), R("rneg", 0, e), R("hk" + b, 0, e), 0.0, A.add, A.max)
+            ts(R("no" + b, 0, n), R("hs" + b, 15, e, 16), -2000.0, None, A.is_lt)
+            tt(R("w" + b, 0, n), R("lk" + b, 0, e, 16), R("no" + b, 0, n), A.mult)
+            group(R("pl" + l, 0, n), [(R("ih", 0, 128), R("c17", 0, n)), (R("ih", 0, 128), R("hs" + b, 15, e, 16)),
+                                      (R("i84h", 0, 128), R("no" + b, 0, n)), (R("nif", 0, 128), R("w" + b, 0, n))])
+            scan(R("ls" + b, 0, e), R("rpos", 0, e), R("lk" + b, 0, e), 0.0, A.add, A.min, half=False)
+            copy(R("hl" + b, 0, n), R("pl" + l, 0, n))
+            tt(R("lof" + gp, i0, i1), R("pl" + l, 0, n), R("ls" + b, 15, e, 16), A.min)
+            copy(R("hl" + b, P, P + n), R("lof" + gp, i0, i1))
+
+        def values(c, i0, i1, n, e, b, l):
+            ch[0] = c
+            for j, (s0, s1) in enumerate(SUB.get(c, [(0, n)])):
+                f0, f1 = 16 * s0, 16 * s1
+                for name, h0, by in (("xh" + b, 0, XHV), ("xl" + b, P, XLV)):
+                    src = IND(R("xb", 0, B), R("hl" + b, h0 + s0, h0 + s1))
+                    if (c, j) in by:
+                        copy(R(name, f0, f1), src, n=f1 - f0)
+                    else:
+                        act(R(name, f0, f1), src, AF.Copy, n=f1 - f0)
+                for c0 in range(f0, f1, 512):
+                    d = "pd%d" % (pieces[0] % 3)
+                    pieces[0] += 1
+                    c1 = min(f1, c0 + 512)
+                    group(R(d, 0, c1 - c0), [(R("nib", 0, 128), R("xh" + b, c0, c1)), (R("ib", 0, 128), R("xl" + b, c0, c1))])
+                    act(R("ad" + b, c0, c1), R(d, 0, c1 - c0), AF.Abs)
+            group(R("pq", 0, n), [(R("l1", 15 - r_, 143 - r_), R("ad" + b, r_, e, 16)) for r_ in range(16)])
+            act(R("r" + gp, i0, i1), R("pq", 0, n), AF.Relu, bias="nb%d" % t, scale=8192.0)
+            scan(R("mn" + b, 0, e), R("rpos", 0, e), R("xh" + b, 0, e), 0.0, A.add, A.min)
+            scan(R("ms" + b, 0, e), R("rneg", 0, e), R("xl" + b, 0, e), 0.0, A.add, A.max)
+            group(R("pl" + l, P, P + n), [(R("ib", 0, 128), R("cq", 0, n)), (R("hib", 0, 128), R("mn" + b, 15, e, 16)),
+                                          (R("hib", 0, 128), R("ms" + b, 15, e, 16))])
+            ts(R("xb", B + i0, B + i1), R("pl" + l, P, P + n), MAGIC, -MAGIC, A.add, A.add)
+            if not last:
+                ts(R("n8", i0, i1), R("xb", B + i0, B + i1), "thf", 8192.0, A.is_lt, A.mult)
+            tt(R("fb" + gp, i0, i1), R("r" + gp, i0, i1), R("ab", Y + i0, Y + i1), A.min)
+            tt(R("ab", Y + i0, Y + i1), R("fb" + gp, i0, i1), R("lof" + gp, i0, i1), A.max)
+            if not last:
+                tt(R("kw", B + i0, B + i1), R("ab", Y + i0, Y + i1), R("n8", i0, i1), A.subtract)
+                for u0, u1 in UH:
+                    if u1 == i1:
+                        next_u(t + 1, u0, u1)
+
+        names(*st[0])
+        names(*st[1])
+        for c in range(len(CH)):
+            values(*st[c])
+            if c + 2 < len(CH):
+                names(*st[c + 2])
+        mw = "mw%d" % t
+        ch[0] = 9
+        for j in range(2):
+            m0, m1, c0, c1 = 128 * j, 128 * j + 128, 8 * j, 8 * j + 8
+            ncj = R("nc%d" % j, 0, 128)
+            group(R("pm", 0, 128), [(R("r" + gp, m0, m1), R("g2", 0, 128))])
+            ts(ncj, R("pm", 0, 128), 0.0, None, A.is_le)
+            group(R("pm", 128, 256), [(R("di%d" % j, 0, 128), R("onh", 0, 128))]
+                  + ([(R("nonh", 0, 128), R("nc0", 0, 128))] if j else []) + [(R("mz%d" % j, 0, 128), ncj)])
+            tt(R("om%d" % j, 0, 128), R("pm", 128, 256), R("mask", 0, 128), A.mult)
+            group(R("pm", 256 + c0, 256 + c1), [(R("om%d" % j, 0, 128), R("selh", 0, 8))])
+            copy(R("off", c0, c1), R("pm", 256 + c0, 256 + c1))
+            src, dst = R("xb", B + m0, B + m1), IND(R(mw, 0, 768), R("off", c0, c1))
+            node("V", [lambda src=src, dst=dst: g.vector.tensor_copy(dst[0], src[0])], src[1] + [("off", c0, c1)], [(mw, 0, 768)],
+                 0.06 + 0.003 * (m1 - m0))
+        k = node("G", [lambda t=t, B=B: send(t, B)], [(mw, 0, CAP)], [], 0.3, sem="rl", inc=8)
+        node("R", [None], [], [("xb", B + NP, B + G)], MLAT, sem="ma%d" % t, inc=8, preds=[k])
+        store(T.ya[:, Y:Y + G], R("ab", Y, Y + G))
+        store(T.yx[:, Y:Y + NP], R("xb", B, B + NP))
+        if not last:
+            nt = "nb%d" % (t + 1)
+            ts(R("n8", NP, G), R("xb", B + NP, B + G), "thf", 8192.0, A.is_lt, A.mult, half=True)
+            tt(R("kw", B + NP, B + G), R("ab", Y + NP, Y + G), R("n8", NP, G), A.subtract)
+            group(R("pm", 288, 296), [(R("onh", 0, 128), R("nc%d" % j, 0, 128, 16)) for j in range(2)])
+            node("V", [lambda: g.vector.tensor_reduce(R("cs", 0, 1)[0], T.pm[:, 288:296], AxisListType.X, A.add)],
+                 [("pm", 288, 296)], col("cs"), 0.064)
+            ts(R("ci", 0, 1), R("cs", 0, 1), -1.0, 2048.0, A.mult, A.add)
+            ts(R("cj", 0, 1), R("ci", 0, 1), 15, None, A.bitwise_and)
+            ts(R(nt, 0, 1), R("cj", 0, 1), -8192.0, "ntau", A.mult, A.add)
+        store(T.yx[:, Y + NP:Y + G], R("xb", B + NP, B + G))
+
+    rest = [0.0] * len(nodes)
+    users = [[] for _ in nodes]
+    for k in range(len(nodes) - 1, -1, -1):
+        nd = nodes[k]
+        rest[k] += nd["cost"] + nd["lat"]
+        for p in nd["ps"]:
+            rest[p] = max(rest[p], rest[k] + WAKE)
+            users[p].append(k)
+    left = [len(nd["ps"]) for nd in nodes]
+    ready_at = [0.0] * len(nodes)
+    ready = {q: [] for q in list(queues) + ["R"]}
+    free = {q: 0.0 for q in ready}
+    for k, nd in enumerate(nodes):
+        if not left[k]:
+            ready[nd["q"]].append(k)
+    order = []
+    for k, nd in enumerate(nodes):
+        rest[k] += BK.get(nd["kind"], 0.0)
+    while len(order) < len(nodes):
+        best = None
+        for q, lst in ready.items():
+            if lst:
+                at = max(free[q], min(ready_at[k] for k in lst))
+                if best is None or at < best[0]:
+                    best = (at, q)
+        at, q = best
+        k = max((k for k in ready[q] if ready_at[k] <= at + DELTA), key=lambda k: (rest[k], -k))
+        at = max(at, ready_at[k])
+        ready[q].remove(k)
+        order.append(k)
+        free[q] = at + nodes[k]["cost"]
+        for u in users[k]:
+            ready_at[u] = max(ready_at[u], free[q] + nodes[k]["lat"] + WAKE)
+            left[u] -= 1
+            if not left[u]:
+                ready[nodes[u]["q"]].append(u)
+
+    STATS["end"] = max(free.values())
+
+    count, waited, snap, token = {}, {}, {}, {}
+    known = {q: {} for q in ready}
+    for k in order:
+        nd = nodes[k]
+        q, sem = nd["q"], nd["sem"]
+        kn = known[q]
+        need = {}
+        for p in nd["ps"]:
+            s, n = token[p]
+            if q != "R" and kn.get(s, 0) < n:
+                need[s] = max(need.get(s, 0), n)
+        for s, n in list(need.items()):
+            if any(o != s and snap[(o, m)].get(s, 0) >= n for o, m in need.items()):
+                del need[s]
+        for s, n in need.items():
+            queues[q].wait_ge(T.sem[s], n)
+            waited[s] = max(waited.get(s, 0), n)
+            for o, m in snap[(s, n)].items():
+                kn[o] = max(kn.get(o, 0), m)
+        for fn in nd["fns"]:
+            count[sem] = count.get(sem, 0) + nd["inc"]
+            if fn is not None:
+                call = fn()
+                if sem != "rl":
+                    call.then_inc(T.sem[sem], nd["inc"])
+        n = count[sem]
+        token[k] = (sem, n)
+        snap[(sem, n)] = dict(kn) if q != "R" else {}
+        snap[(sem, n)][sem] = n
+    for s, n in count.items():
+        if waited.get(s, 0) < n:
+            (g if s == "rl" else g.sync).wait_ge(T.sem[s], n)

@@ -6,31 +6,33 @@ G = NP + FO * CAP
 TOT = S + RO * G
 CH = [(0, 64), (64, 128), (128, 192), (192, 256)]
 UH = [(0, 256)]
-XHV, XLV = ((3, 0), (3, 1), (2, 0)), ()
+XHV, XLV = ((2, 0), (3, 0)), ()
+FUS = ((3, 1),)
 SUB = {3: [(0, 32), (32, 64)]}
 P = max(b - a for a, b in CH)
 E = 16 * P
 DEP = 4
+AHEAD = 4
 WAKE = 0.1
 GCY, TCY, MLAT = 1.6, 0.001, 3.0
-DELTA = 0.15
-BK = {'-:9': -10.7, 'ab:0': 3.0, 'ab:1': -3.6, 'ab:2': -7.5, 'ab:3': -3.9, 'ad:0': -5.5, 'ad:1': -2.3, 'ad:2': 6.0, 'ad:3': -6.1,
-      'ci:9': -0.1, 'cj:9': -1.8, 'cs:9': 0.8, 'e:3': -3.6, 'fb:0': 1.8, 'fb:1': 2.2, 'fb:2': 3.0, 'fb:3': -8.0, 'hk:0': 4.4, 'hk:1': 5.5,
-      'hk:2': -5.7, 'hk:3': -10.1, 'hl:0': -3.5, 'hl:1': 0.6, 'hl:2': -2.9, 'hl:3': 9.5, 'hs:0': -0.4, 'hs:1': -3.5, 'hs:2': 0.1,
-      'hs:3': -3.7, 'kw:0': -0.2, 'kw:1': 3.9, 'kw:2': -6.7, 'kw:3': 7.1, 'kw:9': 3.1, 'lk:0': -1.9, 'lk:1': -0.1, 'lk:2': 0.2,
-      'lk:3': 3.9, 'lof:0': -0.4, 'lof:1': 0.7, 'lof:2': -2.1, 'lof:3': 7.8, 'ls:0': -3.3, 'ls:1': -3.7, 'ls:2': -4.9, 'ls:3': -8.8,
-      'mn:0': 7.7, 'mn:1': -6.3, 'mn:2': -7.2, 'mn:3': -5.1, 'ms:0': 3.5, 'ms:1': -2.7, 'ms:2': -16.2, 'ms:3': 0.6, 'mw:9': -0.2,
-      'n:0': -1.6, 'n:1': 1.4, 'n:2': 2.0, 'n:3': 4.5, 'n:9': -6.8, 'nb:9': -6.5, 'nc:9': 7.7, 'no:0': -3.2, 'no:1': -0.1, 'no:2': -2.4,
-      'no:3': -1.3, 'off:9': 1.2, 'om:9': 6.5, 'pd:0': -7.6, 'pd:1': -2.5, 'pd:2': -14.9, 'pd:3': 8.0, 'pl:0': -7.5, 'pl:1': -11.6,
-      'pl:2': -2.2, 'pl:3': 3.9, 'pm:9': 7.7, 'pq:0': -3.0, 'pq:1': -1.6, 'pq:2': 2.1, 'pq:3': 10.3, 'pw:3': -0.7, 'r:0': 3.9, 'r:1': 6.4,
-      'r:2': 3.5, 'r:3': 1.6, 'ui:3': 2.7, 'uj:3': -1.5, 'uo:3': 2.9, 'w:0': 2.0, 'w:1': -3.7, 'w:2': -4.6, 'w:3': -2.9, 'xb:0': 7.8,
-      'xb:1': 5.9, 'xb:2': -5.1, 'xb:3': 1.0, 'xb:9': 2.6, 'xh:0': -3.4, 'xh:1': 3.6, 'xh:2': -3.8, 'xh:3': 4.1, 'xl:0': -6.2,
-      'xl:1': -6.8, 'xl:2': 0.4, 'xl:3': 6.0, 'yf:3': -4.6}
+DELTA = 0.3
+BK = {'-:9': 5.2, 'ab:0': -6.2, 'ab:1': 3.1, 'ab:2': -7.5, 'ab:3': -5.7, 'ad:0': 8.1, 'ad:1': 5.0, 'ad:2': -6.5, 'ad:3': -6.8,
+      'ci:9': -1.5, 'cj:9': -7.0, 'df:3': -2.8, 'e:3': -8.2, 'fb:0': -4.8, 'fb:1': -4.7, 'fb:2': -4.3, 'fb:3': 6.5, 'fc:9': 6.6,
+      'hk:0': 13.4, 'hk:1': 5.9, 'hk:2': -9.1, 'hk:3': -9.8, 'hl:0': -5.7, 'hl:1': 3.6, 'hl:2': 1.2, 'hl:3': 3.7, 'hs:0': 5.6,
+      'hs:1': -9.0, 'hs:2': -2.7, 'hs:3': 2.3, 'kw:0': -7.4, 'kw:1': -3.7, 'kw:2': 4.7, 'kw:3': -4.6, 'kw:9': -1.7, 'lk:0': 7.2,
+      'lk:1': -7.2, 'lk:2': -3.5, 'lk:3': 2.4, 'lof:0': 2.1, 'lof:1': 8.7, 'lof:2': 2.0, 'lof:3': 10.4, 'ls:0': -2.6, 'ls:1': 10.8,
+      'ls:2': -8.2, 'ls:3': -8.5, 'mn:0': -6.4, 'mn:1': -4.8, 'mn:2': -7.1, 'mn:3': -3.1, 'ms:0': -5.5, 'ms:1': -3.6, 'ms:2': -3.8,
+      'ms:3': 7.7, 'mw:9': -4.1, 'nc:9': 4.0, 'no:0': -4.2, 'no:1': 2.4, 'no:2': 5.8, 'no:3': -0.4, 'nq:9': -2.0, 'off:9': -5.0,
+      'pd:0': 12.2, 'pd:1': 5.8, 'pd:2': -2.8, 'pd:3': -8.5, 'pl:0': 6.8, 'pl:1': 5.8, 'pl:2': 3.1, 'pl:3': -5.5, 'pm:9': 9.1, 'pq:0': 1.3,
+      'pq:1': 7.3, 'pq:2': -5.3, 'pq:3': -6.8, 'pw:0': -1.7, 'pw:1': -7.7, 'pw:2': -2.2, 'pw:3': -7.0, 'pw:7': -5.7, 'pw:9': -4.0,
+      'r:0': 10.9, 'r:1': 7.0, 'r:2': -5.4, 'r:3': -5.5, 'ui:3': -10.1, 'uj:3': -6.7, 'uo:3': -1.9, 'w:0': 0.4, 'w:1': 8.0, 'w:2': -2.9,
+      'w:3': 1.0, 'xb:0': 3.9, 'xb:1': 2.2, 'xb:2': -3.3, 'xb:3': -2.5, 'xb:9': -0.7, 'xh:0': -5.3, 'xh:1': -4.6, 'xh:2': -6.7,
+      'xh:3': -8.1, 'xl:0': 7.1, 'xl:1': 5.8, 'xl:2': -1.1, 'xl:3': -2.3, 'yf:3': 6.4}
 STATS = {}
 MAGIC = 12582912.0
 F16 = "float16"
 
-COLS = ["wtf", "thf", "ntau", "prf", "pixf", "cs", "ia0", "ia1", "iz0", "iz1", "nb0", "nb1", "nb2", "nb3"]
+COLS = ["wtf", "thf", "ntau", "prf", "pixf", "cs", "iz0", "iz1", "nb0", "nb1", "nb2", "nb3"]
 
 SCRATCH = {
     "xb": ("sbuf", [128, TOT], "bfloat16"),
@@ -61,9 +63,9 @@ SCRATCH = {
     "c16": ("sbuf", [128, 16], "float32"), "icf": ("sbuf", [128, 16], "float32"),
     "uc": ("sbuf", [128, 16], "float32"),
     "ui": ("sbuf", [128, 16], "int32"), "uj": ("sbuf", [128, 16], "int32"), "uo": ("sbuf", [128, 16], "uint16"),
-    "n8": ("sbuf", [128, G], "bfloat16"),
-    "uut": ("sbuf", [128, 128], "bfloat16"), "qm": ("sbuf", [128, 128], "bfloat16"), "mask": ("sbuf", [128, 128], F16),
-    "onh": ("sbuf", [128, 128], F16), "nonh": ("sbuf", [128, 128], F16), "selh": ("sbuf", [128, 8], F16),
+    "am": ("sbuf", [128, 128], "bfloat16"), "qm": ("sbuf", [128, 128], "bfloat16"), "leq": ("sbuf", [128, 128], F16),
+    "bef": ("sbuf", [128, 8], "bfloat16"), "befh": ("sbuf", [128, 8], F16), "ich": ("sbuf", [128, 16], F16),
+    "onh": ("sbuf", [128, 128], F16), "nonh": ("sbuf", [128, 8], F16), "selh": ("sbuf", [128, 8], F16),
     "pm": ("psum", [128, 512], "float32"),
     "off": ("sbuf", [128, 16], "uint16"),
     "ci": ("sbuf", [128, 1], "int32"), "cj": ("sbuf", [128, 1], "int32"),
@@ -71,8 +73,9 @@ SCRATCH = {
     "pq": ("psum", [128, 512], "float32"), "pw": ("psum", [128, 512], "float32"),
 }
 for _b in range(2):
-    for _n in ("nc", "om", "di", "dz", "mz"):
+    for _n in ("nc", "nq", "qz", "mz"):
         SCRATCH["%s%d" % (_n, _b)] = ("sbuf", [128, 128], F16)
+    SCRATCH["df%d" % _b] = ("sbuf", [128, E], "bfloat16")
     SCRATCH["yf%d" % _b] = ("sbuf", [128, NP], "float32")
     SCRATCH["e16%d" % _b] = ("sbuf", [128, NP], "uint16")
     SCRATCH["r%d" % _b] = ("sbuf", [128, NP], "bfloat16")
@@ -105,7 +108,7 @@ def rank_program(g, core, T, topo):
     queues = {"V": g.vector, "S": g.scalar, "T": g.tensor, "G": g, "Y": g.sync}
     own = {"V": "sv", "S": "ss", "T": "st", "G": "sg"}
     CY = 0.001
-    ch = [8]
+    ch, parts = [8], {}
 
     nodes, acc = [], {}
 
@@ -125,6 +128,10 @@ def rank_program(g, core, T, topo):
 
     def node(q, fns, ins, outs, cost, sem=None, inc=1, preds=(), lat=0.0):
         k, ps = len(nodes), set(preds)
+        early = []
+        for regs in parts.get(k, ()):
+            early.append({a[4] for name, c0, c1 in regs for a in acc.get(name, ()) if clash(a, q, name, c0, c1, False)})
+        before = {a[4] for name, c0, c1 in outs for a in acc.get(name, ()) if clash(a, q, name, c0, c1, True)}
         kind = outs[0][0].strip("0123456789") if outs else "-"
         for regs, w in ((ins, False), (outs, True)):
             for name, c0, c1 in regs:
@@ -137,7 +144,7 @@ def rank_program(g, core, T, topo):
                 if w:
                     lst[:] = [a for a in lst if not (c0 <= a[0] and a[1] <= c1)]
                 lst.append((c0, c1, w, q, k))
-        nodes.append({"q": q, "fns": fns, "cost": cost, "sem": sem or own[q], "inc": inc, "ps": sorted(ps), "lat": lat, "kind": kind + ":%d" % ch[0]})
+        nodes.append({"q": q, "fns": fns, "cost": cost, "sem": sem or own[q], "inc": inc, "ps": sorted(ps), "early": early, "before": before, "lat": lat, "kind": kind + ":%d" % ch[0]})
         return k
 
     def cat(*rs):
@@ -169,9 +176,10 @@ def rank_program(g, core, T, topo):
         else:
             node("V", [lambda: g.vector.tensor_scalar(out[0], in0[0], s1, s2, op0, op1)], ins, out[1], cost)
 
-    def tt(out, in0, in1, op):
+    def tt(out, in0, in1, op, n=None):
         ps = any(x[1][0][0][:2] in ("pl", "pw", "pm") for x in (in0, in1))
-        node("V", [lambda: g.vector.tensor_tensor(out[0], in0[0], in1[0], op)], cat(in0, in1), out[1], size(out) * (1 if ps else 2) * CY)
+        node("V", [lambda: g.vector.tensor_tensor(out[0], in0[0], in1[0], op)], cat(in0, in1), out[1],
+             gat(n) if n else size(out) * (1 if ps else 2) * CY)
 
     def scan(out, d0, d1, init, op0, op1, half=True):
         first, ins = init, cat(d0, d1)
@@ -200,6 +208,7 @@ def rank_program(g, core, T, topo):
     def group(out, pairs):
         fns, ins, cost = [], [], 0.0
         for j, (l, r_) in enumerate(pairs):
+            parts.setdefault(len(nodes), []).append(l[1] + r_[1])
             fns.append(lambda l=l, r_=r_, j=j: g.tensor.matmul(out[0], l[0], r_[0], j == 0, j == len(pairs) - 1))
             ins += [x for x in l[1] + r_[1] if x not in ins]
             cost += max(64, out[1][0][2] - out[1][0][1]) * TCY * (4 if l[1][0][0] == "nif" else 1)
@@ -211,13 +220,12 @@ def rank_program(g, core, T, topo):
     def load(q, pairs, sem, outs, lat):
         node(q, [lambda o=o, i=i: queues[q].dma_start(o, i) for o, i in pairs], [], outs, 0.06 * len(pairs), sem=sem, inc=16, lat=lat)
 
+    load("Y", [(T.wti[:, 0:1], T.wt[:, 0:1])], "lc0", col("wti"), 2.0)
     load("Y", [(T.thi[:, 0:1], T.th[:, 0:1])], "lc1", col("thi"), 2.0)
-    load("S", [(T.wti[:, 0:1], T.wt[:, 0:1])], "lc0", col("wti"), 2.0)
-    for j, b in enumerate((3, 0, 1, 2)):
-        load("Y", [(T.xb[:, 512 * b:512 * b + 512], T.x0[:, 512 * b:512 * b + 512])], "lx%d" % b,
-             [("xb", 512 * b, 512 * b + 512)], 2.5 + 0.8 * j)
-    load("S", [(T.kdw[16 * k:16 * k + 16, :], T.kd[:, :]) for k in range(8)], "lk", [("kdw", 0, U)], 10.0)
-    load("Y", [(T.taui[:, 0:1], T.tau[:, 0:1])], "lc2", col("taui"), 6.0)
+    for j, (c0, c1) in enumerate(((1536, 2048), (0, 768), (768, 1536))):
+        load("Y", [(T.xb[:, c0:c1], T.x0[:, c0:c1])], "lx%d" % j, [("xb", c0, c1)], 2.5 + 0.8 * j)
+    load("Y", [(T.kdw[16 * k:16 * k + 16, :], T.kd[:, :]) for k in range(8)], "lk", [("kdw", 0, U)], 9.5)
+    load("Y", [(T.taui[:, 0:1], T.tau[:, 0:1])], "lc2", col("taui"), 9.5)
 
     fill(R("onesb", 0, 512), 1.0)
 
@@ -233,7 +241,8 @@ def rank_program(g, core, T, topo):
     asel(R("l1", 0, 144), R("g2", 0, 144), [[0, 9], [1, 16]], A.is_equal, -15, 0)
     node("G", [lambda: g.iota(T.pix[:, 0:1], [[0, 1]], 0, 1)], [], col("pix"), 0.15)
     iota("c16", 0, 16, [[16, 16]], 0, 0)
-    asel(R("uut", 0, 128), R("onesb", 0, 128), [[1, 128]], A.is_ge, 0, -1)
+    asel(R("am", 0, 128), R("onesb", 0, 128), [[0, 8], [-1, 16]], A.is_ge, 0, 1)
+    asel(R("bef", 0, 8), R("onesb", 0, 8), [[16, 8]], A.is_gt, 0, -1)
     asel(R("qm", 0, 128), R("onesb", 0, 128), [[0, 8], [-1, 16]], A.is_equal, 0, 1)
     for b in range(3):
         iota("ab", 512 * b, 512 * b + 512, [[1, 512]], S + 512 * b, 0)
@@ -252,8 +261,8 @@ def rank_program(g, core, T, topo):
         B = S + G * t
         c0, c1 = i0 // 16, i1 // 16
         n = str(t % 2)
-        wrap(R("pw", c0, c1), "lw", "xb", B - G + i0, B - G + i1)
-        tt(R("ui", c0, c1), R("pw", c0, c1), R("uc", c0, c1), A.add)
+        wrap(R("pq", 304 + c0, 304 + c1), "lw", "xb", B - G + i0, B - G + i1)
+        tt(R("ui", c0, c1), R("pq", 304 + c0, 304 + c1), R("uc", c0, c1), A.add)
         ts(R("uj", c0, c1), R("ui", c0, c1), 4095, None, A.bitwise_and)
         copy(R("uo", c0, c1), R("uj", c0, c1))
         ts(R("yf" + n, i0, i1), IND(R("kdw", 0, U), R("uo", c0, c1)), B / 4096.0, -0.484375, A.mult, A.add, n=i1 - i0)
@@ -280,17 +289,18 @@ def rank_program(g, core, T, topo):
     copy(R("nb0", 0, 1), R("ntau", 0, 1))
     copy(R("pixf", 0, 1), R("pix", 0, 1))
     copy(R("onh", 0, 128), R("onesb", 0, 128))
-    ts(R("nonh", 0, 128), R("onesb", 0, 128), -1.0, None, A.mult)
+    ts(R("nonh", 0, 8), R("onesb", 0, 8), -1.0, None, A.mult)
+    ts(R("befh", 0, 8), R("bef", 0, 8), -1.0, None, A.mult)
+    copy(R("ich", 0, 16), R("icf", 0, 16))
     group(R("pm", 0, 128), [(R("qm", 0, 128), R("qm", 0, 128))])
-    copy(R("mask", 0, 128), R("pm", 0, 128))
+    group(R("pm", 128, 256), [(R("am", 0, 128), R("qm", 0, 128))])
     copy(R("selh", 0, 8), R("g2", 0, 128, 16))
+    copy(R("leq", 0, 128), R("pm", 128, 256))
     for j in range(2):
         n = str(j)
-        ts(R("ia" + n, 0, 1), R("pixf", 0, 1), 128.0 * j, None, A.add)
         ts(R("iz" + n, 0, 1), R("pixf", 0, 1), 256.0 + 128.0 * j, None, A.add)
-        ts(R("di" + n, 0, 128), R("ih", 0, 128), "ia" + n, None, A.mult)
-        ts(R("dz" + n, 0, 128), R("ih", 0, 128), "iz" + n, None, A.mult)
-        tt(R("mz" + n, 0, 128), R("dz" + n, 0, 128), R("uut", 0, 128), A.subtract)
+        ts(R("mz" + n, 0, 128), R("pm", 0, 128), "iz" + n, None, A.mult)
+        tt(R("qz" + n, 0, 128), R("mz" + n, 0, 128), R("leq", 0, 128), A.subtract)
     for t in range(RO):
         fill(R("mw%d" % t, 0, CAP), 0.0)
 
@@ -342,16 +352,21 @@ def rank_program(g, core, T, topo):
             ch[0] = c
             for j, (s0, s1) in enumerate(SUB.get(c, [(0, n)])):
                 f0, f1 = 16 * s0, 16 * s1
-                for name, h0, by in (("xh" + b, 0, XHV), ("xl" + b, P, XLV)):
+                for name, h0, by in (("xl" + b, P, XLV), ("xh" + b, 0, XHV)):
                     src = IND(R("xb", 0, B), R("hl" + b, h0 + s0, h0 + s1))
                     if (c, j) in by:
                         copy(R(name, f0, f1), src, n=f1 - f0)
                     else:
                         act(R(name, f0, f1), src, AF.Copy, n=f1 - f0)
+                if (c, j) in FUS:
+                    tt(R("df" + l, f0, f1), IND(R("xb", 0, B), R("hl" + b, s0, s1)), R("xl" + b, f0, f1), A.subtract, n=f1 - f0)
+                    act(R("ad" + b, f0, f1), R("df" + l, f0, f1), AF.Abs)
+                    continue
                 for c0 in range(f0, f1, 512):
                     d = "pd%d" % (pieces[0] % 3)
                     pieces[0] += 1
                     c1 = min(f1, c0 + 512)
+                    assert c1 > c0
                     group(R(d, 0, c1 - c0), [(R("nib", 0, 128), R("xh" + b, c0, c1)), (R("ib", 0, 128), R("xl" + b, c0, c1))])
                     act(R("ad" + b, c0, c1), R(d, 0, c1 - c0), AF.Abs)
             group(R("pq", 0, n), [(R("l1", 15 - r_, 143 - r_), R("ad" + b, r_, e, 16)) for r_ in range(16)])
@@ -362,21 +377,23 @@ def rank_program(g, core, T, topo):
                                           (R("hib", 0, 128), R("ms" + b, 15, e, 16))])
             ts(R("xb", B + i0, B + i1), R("pl" + l, P, P + n), MAGIC, -MAGIC, A.add, A.add)
             if not last:
-                ts(R("n8", i0, i1), R("xb", B + i0, B + i1), "thf", 8192.0, A.is_lt, A.mult)
-            tt(R("fb" + gp, i0, i1), R("r" + gp, i0, i1), R("ab", Y + i0, Y + i1), A.min)
+                ts(R("pw", i0, i1), R("xb", B + i0, B + i1), "thf", 8192.0, A.is_lt, A.mult)
+            tt(R("fb" + gp, i0, i1), R("r" + gp, i0, i1), R("pw", NP + i0, NP + i1), A.min)
             tt(R("ab", Y + i0, Y + i1), R("fb" + gp, i0, i1), R("lof" + gp, i0, i1), A.max)
             if not last:
-                tt(R("kw", B + i0, B + i1), R("ab", Y + i0, Y + i1), R("n8", i0, i1), A.subtract)
+                tt(R("kw", B + i0, B + i1), R("ab", Y + i0, Y + i1), R("pw", i0, i1), A.subtract)
                 for u0, u1 in UH:
                     if u1 == i1:
                         next_u(t + 1, u0, u1)
 
-        names(*st[0])
-        names(*st[1])
+        ch[0] = 7
+        act(R("pw", NP, 2 * NP), R("ab", Y, Y + NP), AF.Copy)
+        for c in range(AHEAD):
+            names(*st[c])
         for c in range(len(CH)):
             values(*st[c])
-            if c + 2 < len(CH):
-                names(*st[c + 2])
+            if c + AHEAD < len(CH):
+                names(*st[c + AHEAD])
         mw = "mw%d" % t
         ch[0] = 9
         for j in range(2):
@@ -384,10 +401,10 @@ def rank_program(g, core, T, topo):
             ncj = R("nc%d" % j, 0, 128)
             group(R("pm", 0, 128), [(R("r" + gp, m0, m1), R("g2", 0, 128))])
             ts(ncj, R("pm", 0, 128), 0.0, None, A.is_le)
-            group(R("pm", 128, 256), [(R("di%d" % j, 0, 128), R("onh", 0, 128))]
-                  + ([(R("nonh", 0, 128), R("nc0", 0, 128))] if j else []) + [(R("mz%d" % j, 0, 128), ncj)])
-            tt(R("om%d" % j, 0, 128), R("pm", 128, 256), R("mask", 0, 128), A.mult)
-            group(R("pm", 256 + c0, 256 + c1), [(R("om%d" % j, 0, 128), R("selh", 0, 8))])
+            tt(R("nq%d" % j, 0, 128), ncj, R("qz%d" % j, 0, 128), A.mult)
+            group(R("pm", 256 + c0, 256 + c1), [(R("ih", 0, 128), R("ich", c0, c1))]
+                  + ([(R("nc0", 0, 128), R("nonh", 0, 8))] if j else [])
+                  + [(ncj, R("befh", 0, 8)), (R("nq%d" % j, 0, 128), R("selh", 0, 8))])
             copy(R("off", c0, c1), R("pm", 256 + c0, 256 + c1))
             src, dst = R("xb", B + m0, B + m1), IND(R(mw, 0, 768), R("off", c0, c1))
             node("V", [lambda src=src, dst=dst: g.vector.tensor_copy(dst[0], src[0])], src[1] + [("off", c0, c1)], [(mw, 0, 768)],
@@ -398,8 +415,8 @@ def rank_program(g, core, T, topo):
         store(T.yx[:, Y:Y + NP], R("xb", B, B + NP))
         if not last:
             nt = "nb%d" % (t + 1)
-            ts(R("n8", NP, G), R("xb", B + NP, B + G), "thf", 8192.0, A.is_lt, A.mult, half=True)
-            tt(R("kw", B + NP, B + G), R("ab", Y + NP, Y + G), R("n8", NP, G), A.subtract)
+            ts(R("pw", 0, 128), R("xb", B + NP, B + G), "thf", 8192.0, A.is_lt, A.mult)
+            tt(R("kw", B + NP, B + G), R("ab", Y + NP, Y + G), R("pw", 0, 128), A.subtract)
             group(R("pm", 288, 296), [(R("onh", 0, 128), R("nc%d" % j, 0, 128, 16)) for j in range(2)])
             node("V", [lambda: g.vector.tensor_reduce(R("cs", 0, 1)[0], T.pm[:, 288:296], AxisListType.X, A.add)],
                  [("pm", 288, 296)], col("cs"), 0.064)
@@ -426,6 +443,8 @@ def rank_program(g, core, T, topo):
     order = []
     for k, nd in enumerate(nodes):
         rest[k] += BK.get(nd["kind"], 0.0)
+        if nd["q"] == "Y" and nd["kind"][-1] == "8":
+            rest[k] = 1e6 - k
     while len(order) < len(nodes):
         best = None
         for q, lst in ready.items():
@@ -453,20 +472,22 @@ def rank_program(g, core, T, topo):
         nd = nodes[k]
         q, sem = nd["q"], nd["sem"]
         kn = known[q]
-        need = {}
-        for p in nd["ps"]:
-            s, n = token[p]
-            if q != "R" and kn.get(s, 0) < n:
-                need[s] = max(need.get(s, 0), n)
-        for s, n in list(need.items()):
-            if any(o != s and snap[(o, m)].get(s, 0) >= n for o, m in need.items()):
-                del need[s]
-        for s, n in need.items():
-            queues[q].wait_ge(T.sem[s], n)
-            waited[s] = max(waited.get(s, 0), n)
-            for o, m in snap[(s, n)].items():
-                kn[o] = max(kn.get(o, 0), m)
-        for fn in nd["fns"]:
+        for j, fn in enumerate(nd["fns"]):
+            need, ps = {}, set() if j else set(nd["ps"])
+            if nd["early"]:
+                ps = nd["early"][j] if j else nd["before"] | nd["early"][0]
+            for p in ps:
+                s, n = token[p]
+                if q != "R" and kn.get(s, 0) < n:
+                    need[s] = max(need.get(s, 0), n)
+            for s, n in list(need.items()):
+                if any(o != s and snap[(o, m)].get(s, 0) >= n for o, m in need.items()):
+                    del need[s]
+            for s, n in need.items():
+                queues[q].wait_ge(T.sem[s], n)
+                waited[s] = max(waited.get(s, 0), n)
+                for o, m in snap[(s, n)].items():
+                    kn[o] = max(kn.get(o, 0), m)
             count[sem] = count.get(sem, 0) + nd["inc"]
             if fn is not None:
                 call = fn()

from concourse.bass import DstId, RemoteDMATransfer
from concourse.mybir import AluOpType, ActivationFunctionType, AxisListType

N, S, U, NP, CAP, FO, RO = 8, 2048, 4096, 256, 64, 2, 4
G = NP + FO * CAP
TOT = S + RO * G
CH = [(0, 64), (64, 128), (128, 192), (192, 256)]
UH = [(0, 256)]
XHV, XLV = ((2, 0), (3, 0)), ()
FUS = ((3, 1),)
SUB = {3: [(0, 32), (32, 64)]}
P = max(b - a for a, b in CH)
E = 16 * P
DEP = 4
AHEAD = 4
WAKE = 0.1
GCY, TCY, MLAT = 1.6, 0.001, 3.0
DELTA = 0.3
BK = {'-:9': 5.2, 'ab:0': -6.2, 'ab:1': 3.1, 'ab:2': -7.5, 'ab:3': -5.7, 'ad:0': 8.1, 'ad:1': 5.0, 'ad:2': -6.5, 'ad:3': -6.8,
      'ci:9': -1.5, 'cj:9': -7.0, 'df:3': -2.8, 'e:3': -8.2, 'fb:0': -4.8, 'fb:1': -4.7, 'fb:2': -4.3, 'fb:3': 6.5, 'fc:9': 6.6,
      'hk:0': 13.4, 'hk:1': 5.9, 'hk:2': -9.1, 'hk:3': -9.8, 'hl:0': -5.7, 'hl:1': 3.6, 'hl:2': 1.2, 'hl:3': 3.7, 'hs:0': 5.6,
      'hs:1': -9.0, 'hs:2': -2.7, 'hs:3': 2.3, 'kw:0': -7.4, 'kw:1': -3.7, 'kw:2': 4.7, 'kw:3': -4.6, 'kw:9': -1.7, 'lk:0': 7.2,
      'lk:1': -7.2, 'lk:2': -3.5, 'lk:3': 2.4, 'lof:0': 2.1, 'lof:1': 8.7, 'lof:2': 2.0, 'lof:3': 10.4, 'ls:0': -2.6, 'ls:1': 10.8,
      'ls:2': -8.2, 'ls:3': -8.5, 'mn:0': -6.4, 'mn:1': -4.8, 'mn:2': -7.1, 'mn:3': -3.1, 'ms:0': -5.5, 'ms:1': -3.6, 'ms:2': -3.8,
      'ms:3': 7.7, 'mw:9': -4.1, 'nc:9': 4.0, 'no:0': -4.2, 'no:1': 2.4, 'no:2': 5.8, 'no:3': -0.4, 'nq:9': -2.0, 'off:9': -5.0,
      'pd:0': 12.2, 'pd:1': 5.8, 'pd:2': -2.8, 'pd:3': -8.5, 'pl:0': 6.8, 'pl:1': 5.8, 'pl:2': 3.1, 'pl:3': -5.5, 'pm:9': 9.1, 'pq:0': 1.3,
      'pq:1': 7.3, 'pq:2': -5.3, 'pq:3': -6.8, 'pw:0': -1.7, 'pw:1': -7.7, 'pw:2': -2.2, 'pw:3': -7.0, 'pw:7': -5.7, 'pw:9': -4.0,
      'r:0': 10.9, 'r:1': 7.0, 'r:2': -5.4, 'r:3': -5.5, 'ui:3': -10.1, 'uj:3': -6.7, 'uo:3': -1.9, 'w:0': 0.4, 'w:1': 8.0, 'w:2': -2.9,
      'w:3': 1.0, 'xb:0': 3.9, 'xb:1': 2.2, 'xb:2': -3.3, 'xb:3': -2.5, 'xb:9': -0.7, 'xh:0': -5.3, 'xh:1': -4.6, 'xh:2': -6.7,
      'xh:3': -8.1, 'xl:0': 7.1, 'xl:1': 5.8, 'xl:2': -1.1, 'xl:3': -2.3, 'yf:3': 6.4}
STATS = {}
MAGIC = 12582912.0
F16 = "float16"

COLS = ["wtf", "thf", "ntau", "prf", "pixf", "cs", "iz0", "iz1", "nb0", "nb1", "nb2", "nb3"]

SCRATCH = {
    "xb": ("sbuf", [128, TOT], "bfloat16"),
    "kw": ("sbuf", [128, TOT], "float32"),
    "kdw": ("sbuf", [128, U], "int32"),
    "ab": ("sbuf", [128, RO * G], "float32"),
    "onesb": ("sbuf", [128, 512], "bfloat16"),
    "io16": ("sbuf", [128, 512], F16),
    "n8h": ("sbuf", [128, S], F16),
    "rneg": ("sbuf", [128, E], "bfloat16"),
    "rpos": ("sbuf", [128, E], "bfloat16"),
    "g2a": ("sbuf", [128, 144], "bfloat16"),
    "g2": ("sbuf", [128, 144], "bfloat16"),
    "l1": ("sbuf", [128, 144], "bfloat16"),
    "lw": ("sbuf", [128, 144], "bfloat16"),
    "ib": ("sbuf", [128, 128], "bfloat16"),
    "nib": ("sbuf", [128, 128], "bfloat16"),
    "hib": ("sbuf", [128, 128], "bfloat16"),
    "nif": ("sbuf", [128, 128], "float32"),
    "ih": ("sbuf", [128, 128], F16),
    "nih": ("sbuf", [128, 128], F16),
    "i84h": ("sbuf", [128, 128], F16),
    "c17": ("sbuf", [128, P], F16),
    "cq": ("sbuf", [128, P], "bfloat16"),
    "wti": ("sbuf", [128, 1], "int32"), "thi": ("sbuf", [128, 1], "int32"), "taui": ("sbuf", [128, 1], "int32"),
    "fc": ("sbuf", [128, len(COLS)], "float32"),
    "pix": ("sbuf", [128, 1], "int32"), "pr": ("sbuf", [128, 1], "int32"),
    "c16": ("sbuf", [128, 16], "float32"), "icf": ("sbuf", [128, 16], "float32"),
    "uc": ("sbuf", [128, 16], "float32"),
    "ui": ("sbuf", [128, 16], "int32"), "uj": ("sbuf", [128, 16], "int32"), "uo": ("sbuf", [128, 16], "uint16"),
    "am": ("sbuf", [128, 128], "bfloat16"), "qm": ("sbuf", [128, 128], "bfloat16"), "leq": ("sbuf", [128, 128], F16),
    "bef": ("sbuf", [128, 8], "bfloat16"), "befh": ("sbuf", [128, 8], F16), "ich": ("sbuf", [128, 16], F16),
    "onh": ("sbuf", [128, 128], F16), "nonh": ("sbuf", [128, 8], F16), "selh": ("sbuf", [128, 8], F16),
    "pm": ("psum", [128, 512], "float32"),
    "off": ("sbuf", [128, 16], "uint16"),
    "ci": ("sbuf", [128, 1], "int32"), "cj": ("sbuf", [128, 1], "int32"),
    "pl0": ("psum", [128, 512], "float32"), "pl1": ("psum", [128, 512], "float32"),
    "pq": ("psum", [128, 512], "float32"), "pw": ("psum", [128, 512], "float32"),
}
for _b in range(2):
    for _n in ("nc", "nq", "qz", "mz"):
        SCRATCH["%s%d" % (_n, _b)] = ("sbuf", [128, 128], F16)
    SCRATCH["df%d" % _b] = ("sbuf", [128, E], "bfloat16")
    SCRATCH["yf%d" % _b] = ("sbuf", [128, NP], "float32")
    SCRATCH["e16%d" % _b] = ("sbuf", [128, NP], "uint16")
    SCRATCH["r%d" % _b] = ("sbuf", [128, NP], "bfloat16")
    SCRATCH["lof%d" % _b] = ("sbuf", [128, NP], "float32")
    SCRATCH["fb%d" % _b] = ("sbuf", [128, NP], "float32")
for _b in range(DEP):
    SCRATCH["hk%d" % _b] = ("sbuf", [128, E], F16)
    SCRATCH["hs%d" % _b] = ("sbuf", [128, E], F16)
    SCRATCH["lk%d" % _b] = ("sbuf", [128, E], "float32")
    SCRATCH["ls%d" % _b] = ("sbuf", [128, E], "float32")
    for _n in ("xl", "xh", "ms", "mn", "ad"):
        SCRATCH["%s%d" % (_n, _b)] = ("sbuf", [128, E], "bfloat16")
    SCRATCH["no%d" % _b] = ("sbuf", [128, P], F16)
    SCRATCH["w%d" % _b] = ("sbuf", [128, P], "float32")
    SCRATCH["hl%d" % _b] = ("sbuf", [128, 2 * P], "uint16")
for _t in range(RO):
    if _t < 3:
        SCRATCH["pd%d" % _t] = ("psum", [128, 512], "float32")
    SCRATCH["mw%d" % _t] = ("sbuf", [128, 768], "bfloat16")

SEMAPHORES = (["sv", "ss", "st", "sg", "rl"] + ["ma%d" % t for t in range(RO)] + ["lx%d" % b for b in range(4)]
              + ["lk"] + ["lc%d" % b for b in range(3)] + ["out%d" % b for b in range(24)])


def rank_program(g, core, T, topo):
    rank = T.rank_of(core)
    if rank is None:
        return
    A, AF = AluOpType, ActivationFunctionType
    queues = {"V": g.vector, "S": g.scalar, "T": g.tensor, "G": g, "Y": g.sync}
    own = {"V": "sv", "S": "ss", "T": "st", "G": "sg"}
    CY = 0.001
    ch, parts = [8], {}

    nodes, acc = [], {}

    def R(name, c0, c1, step=1):
        if name in COLS:
            k = COLS.index(name)
            return (T.fc[:, k:k + 1], [("fc", k, k + 1)])
        return (T[name][:, c0:c1:step] if step > 1 else T[name][:, c0:c1], [(name, c0, c1)])

    def IND(win, off):
        return (win[0].indirect(off[0]), win[1] + off[1])

    def clash(a, q, name, c0, c1, w):
        if a[0] < c1 and c0 < a[1] and (w or a[2]):
            return True
        return name[:2] in ("pd", "pl", "pq", "pw", "pm") and a[3] != q

    def node(q, fns, ins, outs, cost, sem=None, inc=1, preds=(), lat=0.0):
        k, ps = len(nodes), set(preds)
        early = []
        for regs in parts.get(k, ()):
            early.append({a[4] for name, c0, c1 in regs for a in acc.get(name, ()) if clash(a, q, name, c0, c1, False)})
        before = {a[4] for name, c0, c1 in outs for a in acc.get(name, ()) if clash(a, q, name, c0, c1, True)}
        kind = outs[0][0].strip("0123456789") if outs else "-"
        for regs, w in ((ins, False), (outs, True)):
            for name, c0, c1 in regs:
                for a in acc.get(name, ()):
                    if a[4] != k and clash(a, q, name, c0, c1, w):
                        ps.add(a[4])
        for regs, w in ((ins, False), (outs, True)):
            for name, c0, c1 in regs:
                lst = acc.setdefault(name, [])
                if w:
                    lst[:] = [a for a in lst if not (c0 <= a[0] and a[1] <= c1)]
                lst.append((c0, c1, w, q, k))
        nodes.append({"q": q, "fns": fns, "cost": cost, "sem": sem or own[q], "inc": inc, "ps": sorted(ps), "early": early, "before": before, "lat": lat, "kind": kind + ":%d" % ch[0]})
        return k

    def cat(*rs):
        return [x for r_ in rs for x in r_[1]]

    def col(c):
        return R(c, 0, 1)[1]

    def gat(n):
        return 0.06 + n * GCY * CY

    def size(r_, j=0):
        return max(64, r_[1][j][2] - r_[1][j][1])

    def copy(out, in_, n=None):
        node("V", [lambda: g.vector.tensor_copy(out[0], in_[0])], in_[1], out[1], gat(n) if n else size(out) * CY)

    def ts(out, in0, s1, s2, op0, op1=None, n=None, half=False):
        ins = list(in0[1])
        if isinstance(s1, str):
            ins += col(s1)
            s1 = R(s1, 0, 1)[0]
        if isinstance(s2, str):
            ins += col(s2)
            s2 = R(s2, 0, 1)[0]
        cost = gat(n) if n else (max(64, size(out) / 2) if half else size(out)) * CY
        if op1 is None:
            node("V", [lambda: g.vector.tensor_scalar(out[0], in0[0], s1, None, op0)], ins, out[1], cost)
        else:
            node("V", [lambda: g.vector.tensor_scalar(out[0], in0[0], s1, s2, op0, op1)], ins, out[1], cost)

    def tt(out, in0, in1, op, n=None):
        ps = any(x[1][0][0][:2] in ("pl", "pw", "pm") for x in (in0, in1))
        node("V", [lambda: g.vector.tensor_tensor(out[0], in0[0], in1[0], op)], cat(in0, in1), out[1],
             gat(n) if n else size(out) * (1 if ps else 2) * CY)

    def scan(out, d0, d1, init, op0, op1, half=True):
        first, ins = init, cat(d0, d1)
        if isinstance(init, tuple):
            first, ins = init[0], ins + init[1]
        node("V", [lambda: g.vector.tensor_tensor_scan(out[0], d0[0], d1[0], first, op0, op1)], ins, out[1],
             max(64, size(out) * (0.5 if half else 1)) * CY)

    def fill(out, c):
        node("V", [lambda: g.vector.memset(out[0], c)], [], out[1], size(out) * 0.5 * CY)

    def act(out, in_, func, bias=None, scale=None, n=None):
        kw, ins = {}, list(in_[1])
        if isinstance(bias, str):
            ins += col(bias)
            kw["bias"] = R(bias, 0, 1)[0]
        elif bias is not None:
            kw["bias"] = bias
        if isinstance(scale, str):
            ins += col(scale)
            kw["scale"] = R(scale, 0, 1)[0]
        elif scale is not None:
            kw["scale"] = scale
        node("S", [lambda: g.scalar.activation(out[0], in_[0], func, **kw)], ins, out[1], gat(n) if n else 0.04 + size(out) * CY)

    def group(out, pairs):
        fns, ins, cost = [], [], 0.0
        for j, (l, r_) in enumerate(pairs):
            parts.setdefault(len(nodes), []).append(l[1] + r_[1])
            fns.append(lambda l=l, r_=r_, j=j: g.tensor.matmul(out[0], l[0], r_[0], j == 0, j == len(pairs) - 1))
            ins += [x for x in l[1] + r_[1] if x not in ins]
            cost += max(64, out[1][0][2] - out[1][0][1]) * TCY * (4 if l[1][0][0] == "nif" else 1)
        node("T", fns, ins, out[1], cost)

    def wrap(out, mat, rname, c0, c1):
        group(out, [(R(mat, 15 - r_, 143 - r_), R(rname, c0 + r_, c1, 16)) for r_ in range(16)])

    def load(q, pairs, sem, outs, lat):
        node(q, [lambda o=o, i=i: queues[q].dma_start(o, i) for o, i in pairs], [], outs, 0.06 * len(pairs), sem=sem, inc=16, lat=lat)

    load("Y", [(T.wti[:, 0:1], T.wt[:, 0:1])], "lc0", col("wti"), 2.0)
    load("Y", [(T.thi[:, 0:1], T.th[:, 0:1])], "lc1", col("thi"), 2.0)
    for j, (c0, c1) in enumerate(((1536, 2048), (0, 768), (768, 1536))):
        load("Y", [(T.xb[:, c0:c1], T.x0[:, c0:c1])], "lx%d" % j, [("xb", c0, c1)], 2.5 + 0.8 * j)
    load("Y", [(T.kdw[16 * k:16 * k + 16, :], T.kd[:, :]) for k in range(8)], "lk", [("kdw", 0, U)], 9.5)
    load("Y", [(T.taui[:, 0:1], T.tau[:, 0:1])], "lc2", col("taui"), 9.5)

    fill(R("onesb", 0, 512), 1.0)

    def asel(out, in_, pattern, op, base, cm):
        node("G", [lambda: g.affine_select(out[0], in_[0], pattern, op, 0.0, base, cm)], in_[1], out[1], 0.5)

    def iota(name, c0, c1, pattern, base, cm):
        node("G", [lambda: g.iota(T[name][:, c0:c1], pattern, base, cm, allow_small_or_imprecise_dtypes=True)], [], [(name, c0, c1)],
             0.15 + 2 * (c1 - c0) * CY)
    asel(R("ib", 0, 128), R("onesb", 0, 128), [[-1, 128]], A.is_equal, 0, 1)
    asel(R("g2a", 0, 144), R("onesb", 0, 144), [[-16, 9], [0, 16]], A.is_ge, 0, 1)
    asel(R("g2", 0, 144), R("g2a", 0, 144), [[16, 9], [0, 16]], A.is_ge, 15, -1)
    asel(R("l1", 0, 144), R("g2", 0, 144), [[0, 9], [1, 16]], A.is_equal, -15, 0)
    node("G", [lambda: g.iota(T.pix[:, 0:1], [[0, 1]], 0, 1)], [], col("pix"), 0.15)
    iota("c16", 0, 16, [[16, 16]], 0, 0)
    asel(R("am", 0, 128), R("onesb", 0, 128), [[0, 8], [-1, 16]], A.is_ge, 0, 1)
    asel(R("bef", 0, 8), R("onesb", 0, 8), [[16, 8]], A.is_gt, 0, -1)
    asel(R("qm", 0, 128), R("onesb", 0, 128), [[0, 8], [-1, 16]], A.is_equal, 0, 1)
    for b in range(3):
        iota("ab", 512 * b, 512 * b + 512, [[1, 512]], S + 512 * b, 0)
    scan(R("io16", 0, 512), R("onesb", 0, 512), R("onesb", 0, 512), -1.0, A.mult, A.add)
    copy(R("ih", 0, 128), R("ib", 0, 128))
    ts(R("nih", 0, 128), R("ib", 0, 128), -1.0, None, A.mult)
    copy(R("thf", 0, 1), R("thi", 0, 1))
    copy(R("wtf", 0, 1), R("wti", 0, 1))
    act(R("lw", 0, 144), R("l1", 0, 144), AF.Copy, scale="wtf")
    ts(R("pr", 0, 1), R("pix", 0, 1), 15, None, A.bitwise_and)
    copy(R("prf", 0, 1), R("pr", 0, 1))
    ts(R("icf", 0, 16), R("c16", 0, 16), "prf", None, A.add)
    ts(R("uc", 0, 16), R("icf", 0, 16), 613.0, None, A.mult)

    def next_u(t, i0, i1):
        B = S + G * t
        c0, c1 = i0 // 16, i1 // 16
        n = str(t % 2)
        wrap(R("pq", 304 + c0, 304 + c1), "lw", "xb", B - G + i0, B - G + i1)
        tt(R("ui", c0, c1), R("pq", 304 + c0, 304 + c1), R("uc", c0, c1), A.add)
        ts(R("uj", c0, c1), R("ui", c0, c1), 4095, None, A.bitwise_and)
        copy(R("uo", c0, c1), R("uj", c0, c1))
        ts(R("yf" + n, i0, i1), IND(R("kdw", 0, U), R("uo", c0, c1)), B / 4096.0, -0.484375, A.mult, A.add, n=i1 - i0)
        ts(R("e16" + n, i0, i1), R("yf" + n, i0, i1), MAGIC, -MAGIC, A.add, A.add)

    for b in (3, 0, 1, 2):
        c0 = 512 * b
        ts(R("n8h", c0, c0 + 512), R("xb", c0, c0 + 512), "thf", 8192.0, A.is_lt, A.mult, half=True)
        group(R("pd%d" % (b % 3), 0, 512), [(R("ih", 0, 128), R("io16", 0, 512)), (R("nih", 0, 128), R("n8h", c0, c0 + 512))])
        act(R("kw", c0, c0 + 512), R("pd%d" % (b % 3), 0, 512), AF.Copy, bias=float(c0))
    for i0, i1 in UH:
        next_u(0, i0, i1)
    fill(R("rneg", 0, E), 0.0)
    fill(R("rpos", 0, E), 0.0)
    fill(R("rneg", 0, E, 16), -32768.0)
    fill(R("rpos", 0, E, 16), 32768.0)
    ts(R("i84h", 0, 128), R("ib", 0, 128), 8448.0, None, A.mult)
    ts(R("c17", 0, P), R("onesb", 0, P), 1792.0, None, A.mult)
    act(R("nif", 0, 128), R("ib", 0, 128), AF.Copy, scale=-1.0)
    act(R("nib", 0, 128), R("ib", 0, 128), AF.Copy, scale=-1.0)
    act(R("hib", 0, 128), R("ib", 0, 128), AF.Copy, scale=0.5)
    fill(R("cq", 0, P), -0.25)
    ts(R("ntau", 0, 1), R("taui", 0, 1), -8192.0, None, A.mult)
    copy(R("nb0", 0, 1), R("ntau", 0, 1))
    copy(R("pixf", 0, 1), R("pix", 0, 1))
    copy(R("onh", 0, 128), R("onesb", 0, 128))
    ts(R("nonh", 0, 8), R("onesb", 0, 8), -1.0, None, A.mult)
    ts(R("befh", 0, 8), R("bef", 0, 8), -1.0, None, A.mult)
    copy(R("ich", 0, 16), R("icf", 0, 16))
    group(R("pm", 0, 128), [(R("qm", 0, 128), R("qm", 0, 128))])
    group(R("pm", 128, 256), [(R("am", 0, 128), R("qm", 0, 128))])
    copy(R("selh", 0, 8), R("g2", 0, 128, 16))
    copy(R("leq", 0, 128), R("pm", 128, 256))
    for j in range(2):
        n = str(j)
        ts(R("iz" + n, 0, 1), R("pixf", 0, 1), 256.0 + 128.0 * j, None, A.add)
        ts(R("mz" + n, 0, 128), R("pm", 0, 128), "iz" + n, None, A.mult)
        tt(R("qz" + n, 0, 128), R("mz" + n, 0, 128), R("leq", 0, 128), A.subtract)
    for t in range(RO):
        fill(R("mw%d" % t, 0, CAP), 0.0)

    outs_used, pieces, uses = [0], [0], [0]

    def store(out, in_):
        node("Y", [lambda: g.sync.dma_start(out, in_[0])], in_[1], [], 0.06, sem="out%d" % outs_used[0], inc=16, lat=2.0)
        outs_used[0] += 1

    def send(t, B):
        trs = []
        for f in range(FO):
            to = T.cores[(rank + 1 + (FO * t + f) % (N - 1)) % N]
            rid, pid, _ = topo.addr(to)
            b = B + NP + CAP * f
            m = 0
            for e in topo.engines(core, to)[4 * f:4 * f + 4]:
                m |= 1 << e
            trs.append(RemoteDMATransfer(dst_ids=[DstId(rid=rid, pnc=pid)], dma_engine_mask=m, remote_sem=T.sem["ma%d" % t],
                                         srcs=[T["mw%d" % t][:, 0:CAP]], dsts=[T.xb[:, b:b + CAP]]))
        g.remote_dma_fused(trs, local_sem=T.sem.rl)

    for t in range(RO):
        B, Y = S + G * t, G * t
        gp = str(t % 2)
        last = t == RO - 1
        st = []
        for c, (i0, i1) in enumerate(CH):
            n, e = i1 - i0, 16 * (i1 - i0)
            st.append((c, i0, i1, n, e, str(uses[0] % DEP), str(uses[0] % 2)))
            uses[0] += 1

        def names(c, i0, i1, n, e, b, l):
            ch[0] = c
            kids = IND(R("kw", 0, B), R("e16" + gp, i0, i1))
            act(R("lk" + b, 0, e), kids, AF.Abs, n=e)
            ts(R("hk" + b, 0, e), kids, -1792.0, -2048.0, A.add, A.max, n=e)
            scan(R("hs" + b, 0, e), R("rneg", 0, e), R("hk" + b, 0, e), 0.0, A.add, A.max)
            ts(R("no" + b, 0, n), R("hs" + b, 15, e, 16), -2000.0, None, A.is_lt)
            tt(R("w" + b, 0, n), R("lk" + b, 0, e, 16), R("no" + b, 0, n), A.mult)
            group(R("pl" + l, 0, n), [(R("ih", 0, 128), R("c17", 0, n)), (R("ih", 0, 128), R("hs" + b, 15, e, 16)),
                                      (R("i84h", 0, 128), R("no" + b, 0, n)), (R("nif", 0, 128), R("w" + b, 0, n))])
            scan(R("ls" + b, 0, e), R("rpos", 0, e), R("lk" + b, 0, e), 0.0, A.add, A.min, half=False)
            copy(R("hl" + b, 0, n), R("pl" + l, 0, n))
            tt(R("lof" + gp, i0, i1), R("pl" + l, 0, n), R("ls" + b, 15, e, 16), A.min)
            copy(R("hl" + b, P, P + n), R("lof" + gp, i0, i1))

        def values(c, i0, i1, n, e, b, l):
            ch[0] = c
            for j, (s0, s1) in enumerate(SUB.get(c, [(0, n)])):
                f0, f1 = 16 * s0, 16 * s1
                for name, h0, by in (("xl" + b, P, XLV), ("xh" + b, 0, XHV)):
                    src = IND(R("xb", 0, B), R("hl" + b, h0 + s0, h0 + s1))
                    if (c, j) in by:
                        copy(R(name, f0, f1), src, n=f1 - f0)
                    else:
                        act(R(name, f0, f1), src, AF.Copy, n=f1 - f0)
                if (c, j) in FUS:
                    tt(R("df" + l, f0, f1), IND(R("xb", 0, B), R("hl" + b, s0, s1)), R("xl" + b, f0, f1), A.subtract, n=f1 - f0)
                    act(R("ad" + b, f0, f1), R("df" + l, f0, f1), AF.Abs)
                    continue
                for c0 in range(f0, f1, 512):
                    d = "pd%d" % (pieces[0] % 3)
                    pieces[0] += 1
                    c1 = min(f1, c0 + 512)
                    assert c1 > c0
                    group(R(d, 0, c1 - c0), [(R("nib", 0, 128), R("xh" + b, c0, c1)), (R("ib", 0, 128), R("xl" + b, c0, c1))])
                    act(R("ad" + b, c0, c1), R(d, 0, c1 - c0), AF.Abs)
            group(R("pq", 0, n), [(R("l1", 15 - r_, 143 - r_), R("ad" + b, r_, e, 16)) for r_ in range(16)])
            act(R("r" + gp, i0, i1), R("pq", 0, n), AF.Relu, bias="nb%d" % t, scale=8192.0)
            scan(R("mn" + b, 0, e), R("rpos", 0, e), R("xh" + b, 0, e), 0.0, A.add, A.min)
            scan(R("ms" + b, 0, e), R("rneg", 0, e), R("xl" + b, 0, e), 0.0, A.add, A.max)
            group(R("pl" + l, P, P + n), [(R("ib", 0, 128), R("cq", 0, n)), (R("hib", 0, 128), R("mn" + b, 15, e, 16)),
                                          (R("hib", 0, 128), R("ms" + b, 15, e, 16))])
            ts(R("xb", B + i0, B + i1), R("pl" + l, P, P + n), MAGIC, -MAGIC, A.add, A.add)
            if not last:
                ts(R("pw", i0, i1), R("xb", B + i0, B + i1), "thf", 8192.0, A.is_lt, A.mult)
            tt(R("fb" + gp, i0, i1), R("r" + gp, i0, i1), R("pw", NP + i0, NP + i1), A.min)
            tt(R("ab", Y + i0, Y + i1), R("fb" + gp, i0, i1), R("lof" + gp, i0, i1), A.max)
            if not last:
                tt(R("kw", B + i0, B + i1), R("ab", Y + i0, Y + i1), R("pw", i0, i1), A.subtract)
                for u0, u1 in UH:
                    if u1 == i1:
                        next_u(t + 1, u0, u1)

        ch[0] = 7
        act(R("pw", NP, 2 * NP), R("ab", Y, Y + NP), AF.Copy)
        for c in range(AHEAD):
            names(*st[c])
        for c in range(len(CH)):
            values(*st[c])
            if c + AHEAD < len(CH):
                names(*st[c + AHEAD])
        mw = "mw%d" % t
        ch[0] = 9
        for j in range(2):
            m0, m1, c0, c1 = 128 * j, 128 * j + 128, 8 * j, 8 * j + 8
            ncj = R("nc%d" % j, 0, 128)
            group(R("pm", 0, 128), [(R("r" + gp, m0, m1), R("g2", 0, 128))])
            ts(ncj, R("pm", 0, 128), 0.0, None, A.is_le)
            tt(R("nq%d" % j, 0, 128), ncj, R("qz%d" % j, 0, 128), A.mult)
            group(R("pm", 256 + c0, 256 + c1), [(R("ih", 0, 128), R("ich", c0, c1))]
                  + ([(R("nc0", 0, 128), R("nonh", 0, 8))] if j else [])
                  + [(ncj, R("befh", 0, 8)), (R("nq%d" % j, 0, 128), R("selh", 0, 8))])
            copy(R("off", c0, c1), R("pm", 256 + c0, 256 + c1))
            src, dst = R("xb", B + m0, B + m1), IND(R(mw, 0, 768), R("off", c0, c1))
            node("V", [lambda src=src, dst=dst: g.vector.tensor_copy(dst[0], src[0])], src[1] + [("off", c0, c1)], [(mw, 0, 768)],
                 0.06 + 0.003 * (m1 - m0))
        k = node("G", [lambda t=t, B=B: send(t, B)], [(mw, 0, CAP)], [], 0.3, sem="rl", inc=8)
        node("R", [None], [], [("xb", B + NP, B + G)], MLAT, sem="ma%d" % t, inc=8, preds=[k])
        store(T.ya[:, Y:Y + G], R("ab", Y, Y + G))
        store(T.yx[:, Y:Y + NP], R("xb", B, B + NP))
        if not last:
            nt = "nb%d" % (t + 1)
            ts(R("pw", 0, 128), R("xb", B + NP, B + G), "thf", 8192.0, A.is_lt, A.mult)
            tt(R("kw", B + NP, B + G), R("ab", Y + NP, Y + G), R("pw", 0, 128), A.subtract)
            group(R("pm", 288, 296), [(R("onh", 0, 128), R("nc%d" % j, 0, 128, 16)) for j in range(2)])
            node("V", [lambda: g.vector.tensor_reduce(R("cs", 0, 1)[0], T.pm[:, 288:296], AxisListType.X, A.add)],
                 [("pm", 288, 296)], col("cs"), 0.064)
            ts(R("ci", 0, 1), R("cs", 0, 1), -1.0, 2048.0, A.mult, A.add)
            ts(R("cj", 0, 1), R("ci", 0, 1), 15, None, A.bitwise_and)
            ts(R(nt, 0, 1), R("cj", 0, 1), -8192.0, "ntau", A.mult, A.add)
        store(T.yx[:, Y + NP:Y + G], R("xb", B + NP, B + G))

    rest = [0.0] * len(nodes)
    users = [[] for _ in nodes]
    for k in range(len(nodes) - 1, -1, -1):
        nd = nodes[k]
        rest[k] += nd["cost"] + nd["lat"]
        for p in nd["ps"]:
            rest[p] = max(rest[p], rest[k] + WAKE)
            users[p].append(k)
    left = [len(nd["ps"]) for nd in nodes]
    ready_at = [0.0] * len(nodes)
    ready = {q: [] for q in list(queues) + ["R"]}
    free = {q: 0.0 for q in ready}
    for k, nd in enumerate(nodes):
        if not left[k]:
            ready[nd["q"]].append(k)
    order = []
    for k, nd in enumerate(nodes):
        rest[k] += BK.get(nd["kind"], 0.0)
        if nd["q"] == "Y" and nd["kind"][-1] == "8":
            rest[k] = 1e6 - k
    while len(order) < len(nodes):
        best = None
        for q, lst in ready.items():
            if lst:
                at = max(free[q], min(ready_at[k] for k in lst))
                if best is None or at < best[0]:
                    best = (at, q)
        at, q = best
        k = max((k for k in ready[q] if ready_at[k] <= at + DELTA), key=lambda k: (rest[k], -k))
        at = max(at, ready_at[k])
        ready[q].remove(k)
        order.append(k)
        free[q] = at + nodes[k]["cost"]
        for u in users[k]:
            ready_at[u] = max(ready_at[u], free[q] + nodes[k]["lat"] + WAKE)
            left[u] -= 1
            if not left[u]:
                ready[nodes[u]["q"]].append(u)

    STATS["end"] = max(free.values())

    count, waited, snap, token = {}, {}, {}, {}
    known = {q: {} for q in ready}
    for k in order:
        nd = nodes[k]
        q, sem = nd["q"], nd["sem"]
        kn = known[q]
        for j, fn in enumerate(nd["fns"]):
            need, ps = {}, set() if j else set(nd["ps"])
            if nd["early"]:
                ps = nd["early"][j] if j else nd["before"] | nd["early"][0]
            for p in ps:
                s, n = token[p]
                if q != "R" and kn.get(s, 0) < n:
                    need[s] = max(need.get(s, 0), n)
            for s, n in list(need.items()):
                if any(o != s and snap[(o, m)].get(s, 0) >= n for o, m in need.items()):
                    del need[s]
            for s, n in need.items():
                queues[q].wait_ge(T.sem[s], n)
                waited[s] = max(waited.get(s, 0), n)
                for o, m in snap[(s, n)].items():
                    kn[o] = max(kn.get(o, 0), m)
            count[sem] = count.get(sem, 0) + nd["inc"]
            if fn is not None:
                call = fn()
                if sem != "rl":
                    call.then_inc(T.sem[sem], nd["inc"])
        n = count[sem]
        token[k] = (sem, n)
        snap[(sem, n)] = dict(kn) if q != "R" else {}
        snap[(sem, n)][sem] = n
    for s, n in count.items():
        if waited.get(s, 0) < n:
            (g if s == "rl" else g.sync).wait_ge(T.sem[s], n)
